import numpy as np
import ml_dtypes


def mxq(x, axis, fmt="e4m3"):
    dtype, down = {"e4m3": (ml_dtypes.float8_e4m3fn, 7), "e5m2": (ml_dtypes.float8_e5m2, 14)}[fmt]
    v = np.moveaxis(np.asarray(x, np.float32).astype(ml_dtypes.bfloat16).astype(np.float64), axis, -1)
    blocks = v.reshape(v.shape[:-1] + (-1, 32))
    amax = np.abs(blocks).max(-1, keepdims=True)
    byte = np.maximum(np.where(amax > 0, np.frexp(amax)[1] - 1 + 127, 0) - down, 1)
    scale = np.exp2(byte - 127.0)
    codes = (blocks / scale).astype(np.float32).astype(dtype).astype(np.float64)
    return np.moveaxis((codes * scale).reshape(v.shape), -1, axis)


WIDE = False


def mx_kscale(k):
    if not WIDE:
        return np.ones(k)
    levels = np.array([24, -24, 12, -12, 0])
    if k % 512:
        return np.exp2(np.random.permutation(np.resize(levels, k // 32))).repeat(32)
    a = np.empty((k // 512, 16))
    for p in range(k // 512):
        a[p, :8] = np.random.permutation(np.resize(levels, 8))
        for g in range(8):
            far = levels[np.abs(levels - a[p, g]) >= 10]
            a[p, g + 8] = far[np.random.randint(len(far))]
    return np.exp2(a.ravel()).repeat(32)


def f64(x):
    return np.asarray(x).astype(np.float64)


def striped(idx):
    return np.tile(idx.reshape(-1, 16).T, (8, 1)).astype(np.uint16)


def unstriped(offs):
    return offs[:16].T.reshape(-1).astype(np.int64)


E2M1 = np.array([0.0, 0.5, 1.0, 1.5, 2.0, 3.0, 4.0, 6.0, -0.0, -0.5, -1.0, -1.5, -2.0, -3.0, -4.0, -6.0])


def pack_weight(w, fmt):
    k, n = w.shape
    w = f64(np.asarray(w, np.float32).astype(ml_dtypes.bfloat16)).reshape(k // 32, 32, n)
    amax = np.abs(w).max(1)
    if fmt == "e4m3":
        byte = np.frexp(amax)[1] - 1 + 127 - 7
    else:
        mant, ex = np.frexp(amax / 6.0)
        byte = np.where(mant > 0.5, ex, ex - 1) + 127
    byte = np.clip(np.where(amax > 0, byte, 1), 1, 254)
    scaled = (w * np.exp2(127.0 - byte)[:, None, :]).reshape(k, n).astype(np.float32)
    by_word = np.ascontiguousarray(scaled.reshape(k // 512, 128, 4, n).transpose(0, 1, 3, 2))
    if fmt == "e4m3":
        words = by_word.astype(ml_dtypes.float8_e4m3fn).view(np.uint8)
    else:
        c = by_word.astype(ml_dtypes.float4_e2m1fn).view(np.uint8) & 0xF
        words = (c[..., 0::2] | (c[..., 1::2] << 4)).reshape(k // 512, 128, 2 * n)
    return np.ascontiguousarray(words), np.ascontiguousarray(byte.astype(np.uint8).reshape(k // 512, 16, n))


def unpack_weight(words, scales, fmt):
    g, _, n = scales.shape
    words = np.ascontiguousarray(words).reshape(g, 128, n, -1)
    if fmt == "e4m3":
        vals = words.view(ml_dtypes.float8_e4m3fn).astype(np.float64)
    else:
        nib = np.empty((g, 128, n, 4), np.uint8)
        nib[..., 0::2] = words & 0xF
        nib[..., 1::2] = words >> 4
        vals = E2M1[nib]
    vals = vals * np.repeat(np.exp2(scales.astype(np.float64) - 127.0), 8, axis=1)[..., None]
    return vals.transpose(0, 1, 3, 2).reshape(g * 512, n)


def pack_table4(v):
    words, scales = pack_weight(v, "e2m1")
    g, t = words.shape[0] // 2, v.shape[1]
    return np.ascontiguousarray(words.reshape(g, 2, 128, t, 2).transpose(0, 2, 3, 1, 4).reshape(g, 128, t, 4)), scales


def unpack_table4(words, scales):
    g, _, t, _ = words.shape
    return unpack_weight(words.reshape(g, 128, t, 2, 2).transpose(0, 3, 1, 2, 4).reshape(2 * g, 128, 2 * t), scales, "e2m1")


def gelu(f):
    return 0.5 * f * (1.0 + np.tanh(np.sqrt(2.0 / np.pi) * (f + 0.044715 * f**3)))


K, L, N, T, J = 1024, 1024, 1024, 4096, 1024


def setup_inputs():
    n = np.random.standard_normal
    s = mx_kscale(K)[:, None]
    s2 = mx_kscale(L)[:, None]
    p_tab = pack_table4(n((K, T)) * s)
    p_wx = pack_weight(n((L, N)) / np.sqrt(L) / s2, "e2m1")
    return {
        "tab_words": p_tab[0],
        "tab_scales": p_tab[1],
        "wt": (n((K, N)) / np.sqrt(K) / s).astype(np.float32),
        "x": (n((L, J)) * s2).astype(np.float32),
        "wx_words": p_wx[0],
        "wx_scales": p_wx[1],
        "b": (0.3 * n(N)).astype(np.float32),
        "offs": striped(np.random.permutation(T)[:J]),
    }


def reference(tab_words, tab_scales, wt, x, wx_words, wx_scales, b, offs):
    idx = unstriped(offs)
    tab_ = unpack_table4(tab_words, tab_scales)[:, idx]
    wt_ = mxq(f64(wt), 0, "e4m3")
    x_q_ = mxq(f64(x), 0, "e4m3")
    x_r_ = mxq(f64(x) - x_q_, 0, "e4m3")
    wx_ = unpack_weight(wx_words, wx_scales, "e2m1")
    y = wt_.T @ tab_ + wx_.T @ x_q_ + wx_.T @ x_r_
    return gelu(y + f64(b)[:, None])

@@ -1,0 +1,287 @@
+from contextlib import ExitStack
+
+import concourse.mybir as mybir
+from concourse.masks import make_identity
+
+K, L, N, T, J = 1024, 1024, 1024, 4096, 1024
+FLOPS = 2 * N * J * (K + 2 * L) + 2 * 512 * L * J
+
+F32 = mybir.dt.float32
+BF16 = mybir.dt.bfloat16
+I32 = mybir.dt.int32
+U32 = mybir.dt.uint32
+U16 = mybir.dt.uint16
+U8 = mybir.dt.uint8
+FP8X4 = mybir.dt.float8_e4m3fn_x4
+FP4X4 = mybir.dt.float4_e2m1fn_x4
+GELU = mybir.ActivationFunctionType.Gelu_apprx_tanh
+SUB = mybir.AluOpType.subtract
+
+P = 128
+PACK = 4
+K_PASS = P * PACK
+PASSES = 2
+HALF = 512
+UNIT = 256
+ACC_BANKS = 6
+
+
+def interleaved(ap):
+    return ap.rearrange("p (c i) t -> p c t i", i=4)
+
+
+def planar(ap):
+    return ap.rearrange("p t (c i) -> p c t i", i=4)
+
+
+def tile_list_tiert_gelu_kernel(
+    tc, tab_words, tab_scales, wt, x, wx_words, wx_scales, b, offs, out
+):
+    nc = tc.nc
+    with ExitStack() as ctx:
+        held = ctx.enter_context(tc.tile_pool(name="held", bufs=1))
+        psum = ctx.enter_context(tc.psum_pool(name="psum", bufs=1))
+        back = ctx.enter_context(tc.psum_pool(name="back", bufs=2))
+
+        def keep(shape, dtype, name):
+            return held.tile(shape, dtype, name=name, align_bytes=64)
+
+        offsets = held.tile([P, J // 16], U16, name="offsets")
+        nc.sync.dma_start(offsets[:], offs)
+
+        scale_window = keep([P, T], U8, "scale_window")
+        nc.sync.dma_start(
+            scale_window[96:P, :].bitcast(I32),
+            tab_scales.rearrange("a q t -> (a q) t").bitcast(I32),
+        )
+        wx_sc = keep([P, PASSES, N], U8, "wx_sc")
+        nc.vector.memset(wx_sc[:].bitcast(I32), 0)
+        b_rows = keep([P, P], F32, "b_rows")
+        nc.vector.memset(b_rows[:], 0.0)
+        nc.vector.memset(scale_window[0:96, :].bitcast(I32), 0)
+        band = keep([P, 7 * P], F32, "band")
+        nc.vector.memset(band[:, 0 : 3 * P], 0.0)
+        nc.vector.memset(band[:, 4 * P :], 0.0)
+        make_identity(nc, band[:, 3 * P : 4 * P])
+        warm = keep([P, 8], F32, "warm")
+        nc.scalar.activation(warm[:, 0:1], band[:, 0:1], GELU)
+        for quad in range(4):
+            nc.sync.dma_start(
+                wx_sc[32 * quad : 32 * quad + 4, :, :].bitcast(I32),
+                wx_scales[:, 4 * quad : 4 * quad + 4, :].rearrange("a r n -> r a n").bitcast(I32),
+            )
+        nc.sync.dma_start(b_rows[0 : N // P, :], b.rearrange("(c p) -> c p", p=P))
+
+        def load_unit(src, a, col0, name):
+            raw = keep([P, PACK, UNIT], F32, name)
+            rows = src[a * K_PASS : (a + 1) * K_PASS, col0 : col0 + UNIT]
+            nc.sync.dma_start(raw[:], rows.rearrange("(p t) w -> p t w", t=PACK))
+            return raw
+
+        x_raw, wt_raw = {}, {}
+
+        def load_x(h):
+            for a in range(PASSES):
+                for q in range(2):
+                    x_raw[h, a, q] = load_unit(x, a, h * HALF + q * UNIT, f"x_raw{h}{a}{q}")
+
+        def load_wt(g):
+            for a in range(PASSES):
+                wt_raw[g, a] = load_unit(wt, a, g * UNIT, f"wt_raw{g}{a}")
+
+        load_x(0)
+        wx_w = keep([P, PASSES, 2 * N], U8, "wx_w")
+        nc.sync.dma_start(wx_w[:].bitcast(I32), wx_words.rearrange("a p c -> p a c").bitcast(I32))
+        load_wt(0)
+        word_window = keep([P, T], U32, "word_window")
+        nc.sync.dma_start(
+            word_window[:].bitcast(I32), tab_words[0].rearrange("p t c -> p (t c)").bitcast(I32)
+        )
+        load_wt(1)
+        load_x(1)
+        load_wt(2)
+        load_wt(3)
+
+        picked_sc = keep([P, J], U8, "picked_sc")
+        nc.vector.tensor_copy(picked_sc[:], scale_window[:].indirect(offsets[:]))
+        tab_sc = []
+        for a in range(PASSES):
+            plane = keep([P, J], U8, f"tab_sc{a}")
+            nc.vector.memset(plane[:].bitcast(I32), 0)
+            for quad in range(4):
+                first = 96 + 16 * a + 4 * quad
+                nc.gpsimd.dma_start(
+                    plane[32 * quad : 32 * quad + 4, :].bitcast(I32),
+                    picked_sc[first : first + 4, :].bitcast(I32),
+                )
+            tab_sc.append(plane)
+
+        eye = keep([P, PACK, P, PACK], BF16, "eye")
+        for t in range(PACK):
+            copy = nc.vector.tensor_copy if t < 2 else nc.scalar.copy
+            copy(
+                interleaved(eye[:, t, :, :]),
+                planar(band[:, (3 - t) * P : (7 - t) * P].rearrange("p (t w) -> p t w", t=PACK)),
+            )
+        eye_w = keep([P, PACK * P], U32, "eye_w")
+        eye_sc = keep([P, PACK * P], U8, "eye_sc")
+        nc.vector.quantize_mx(eye_w[:].bitcast(FP8X4), eye_sc[:], eye[:].rearrange("p t m i -> p (t m i)"))
+
+        b_bank = back.tile([P, PACK, P], F32, name="back_bank")
+        nc.tensor.transpose(b_bank[:, 0, :], b_rows[:], band[:, 3 * P : 4 * P])
+        bias = keep([P, N // P], F32, "bias")
+        nc.scalar.copy(bias[:], b_bank[:, 0, 0 : N // P])
+
+        def cast(raw, name, engine):
+            grouped = keep([P, UNIT, PACK], BF16, name)
+            if engine == "scalar":
+                nc.scalar.copy(interleaved(grouped[:]), planar(raw[:]))
+            else:
+                nc.vector.tensor_copy(interleaved(grouped[:]), planar(raw[:]))
+            return grouped
+
+        def quantize(grouped, words, scales):
+            nc.vector.quantize_mx(words.bitcast(FP8X4), scales, grouped[:].rearrange("p w t -> p (w t)"))
+
+        xq, xr, wq = {}, {}, {}
+
+        def tier_one(h, a):
+            words = keep([P, HALF], U32, f"xq_w{h}{a}")
+            scales = keep([P, HALF], U8, f"xq_sc{h}{a}")
+            xq[h, a] = (words, scales)
+            for q in range(2):
+                cols = slice(q * UNIT, (q + 1) * UNIT)
+                grouped = cast(x_raw[h, a, q], f"x_bf{h}{a}{q}", "scalar")
+                quantize(grouped, words[:, cols], scales[:, cols])
+
+        def tier_two(h, a):
+            q_words, q_scales = xq[h, a]
+            words = keep([P, HALF], U32, f"xr_w{h}{a}")
+            scales = keep([P, HALF], U8, f"xr_sc{h}{a}")
+            xr[h, a] = (words, scales)
+            for q in range(2):
+                left = keep([P, UNIT, PACK], BF16, f"left{h}{a}{q}")
+                for s in range(UNIT // P):
+                    cols = slice(q * UNIT + s * P, q * UNIT + (s + 1) * P)
+                    bank = back.tile([P, PACK, P], F32, name="back_bank")
+                    for t in range(PACK):
+                        nc.tensor.matmul_mx(
+                            bank[:, t, :],
+                            lhsT=eye_w[:, t * P : (t + 1) * P].bitcast(FP8X4),
+                            lhsT_scale=eye_sc[:, t * P : (t + 1) * P],
+                            rhs=q_words[:, cols].bitcast(FP8X4),
+                            rhs_scale=q_scales[:, cols],
+                            start=True,
+                            stop=True,
+                        )
+                    nc.vector.tensor_tensor(
+                        interleaved(left[:, s * P : (s + 1) * P, :]),
+                        planar(x_raw[h, a, q][:, :, s * P : (s + 1) * P]),
+                        planar(bank[:]),
+                        SUB,
+                    )
+                cols = slice(q * UNIT, (q + 1) * UNIT)
+                quantize(left, words[:, cols], scales[:, cols])
+
+        def quantize_wt(g, engine):
+            for a in range(PASSES):
+                words = keep([P, UNIT], U32, f"wt_w{g}{a}")
+                scales = keep([P, UNIT], U8, f"wt_sc{g}{a}")
+                grouped = cast(wt_raw[g, a], f"wt_bf{g}{a}", engine)
+                quantize(grouped, words[:], scales[:])
+                wq[g, a] = (words, scales)
+
+        tab_w = {}
+
+        def gather_words(h):
+            picked = keep([P, HALF], U32, f"picked_w{h}")
+            lists = offsets[:, h * HALF // 16 : (h + 1) * HALF // 16]
+            nc.vector.tensor_copy(picked[:], word_window[:].indirect(lists))
+            parted = keep([P, PASSES, 2 * HALF], U8, f"tab_w{h}")
+            nc.vector.tensor_copy(
+                parted[:].bitcast(U16), picked[:].bitcast(U16).rearrange("p (j d) -> p d j", d=PASSES)
+            )
+            tab_w[h] = parted
+
+        acc, done = {}, {}
+
+        def open_tile(h, n):
+            acc[h, n] = psum.tile([P, HALF], F32, name=f"acc{len(acc) % ACC_BANKS}")
+            done[h, n] = 0
+
+        def add_pass(h, n, lhsT, lhsT_scale, rhs, rhs_scale):
+            count = done[h, n]
+            nc.tensor.matmul_mx(
+                acc[h, n][:], lhsT=lhsT, lhsT_scale=lhsT_scale, rhs=rhs, rhs_scale=rhs_scale,
+                start=count == 0, stop=count == 3 * PASSES - 1,
+            )
+            done[h, n] = count + 1
+            if count == 3 * PASSES - 1:
+                result = keep([P, HALF], F32, f"result{h}{n}")
+                nc.scalar.activation(result[:], acc[h, n][:], GELU, bias=bias[:, n : n + 1])
+                nc.sync.dma_start(out[n * P : (n + 1) * P, h * HALF : (h + 1) * HALF], result[:])
+
+        def x_pass(tier, h, a, n):
+            words, scales = tier[h, a]
+            add_pass(
+                h, n,
+                wx_w[:, a, 2 * n * P : 2 * (n + 1) * P].bitcast(FP4X4), wx_sc[:, a, n * P : (n + 1) * P],
+                words[:].bitcast(FP8X4), scales[:],
+            )
+
+        def x_passes(h, n):
+            for a in range(PASSES):
+                x_pass(xq, h, a, n)
+                x_pass(xr, h, a, n)
+
+        def tab_passes(h, n):
+            for a in range(PASSES):
+                words, scales = wq[n // 2, a]
+                cols = slice(n % 2 * P, (n % 2 + 1) * P)
+                add_pass(
+                    h, n,
+                    words[:, cols].bitcast(FP8X4), scales[:, cols],
+                    tab_w[h][:, a, :].bitcast(FP4X4), tab_sc[a][:, h * HALF : (h + 1) * HALF],
+                )
+
+        for a in range(PASSES):
+            tier_one(0, a)
+            tier_two(0, a)
+        for n in range(ACC_BANKS):
+            open_tile(0, n)
+        for a in range(PASSES):
+            for tier in (xq, xr):
+                for n in range(ACC_BANKS):
+                    x_pass(tier, 0, a, n)
+        quantize_wt(0, "scalar")
+        gather_words(0)
+        for n in (0, 1):
+            tab_passes(0, n)
+        quantize_wt(1, "scalar")
+        gather_words(1)
+        for n in (6, 7):
+            open_tile(0, n)
+            x_passes(0, n)
+        for n in (2, 3):
+            tab_passes(0, n)
+        for a in range(PASSES):
+            tier_one(1, a)
+            tier_two(1, a)
+        for n in (0, 1):
+            open_tile(1, n)
+            tab_passes(1, n)
+        quantize_wt(2, "scalar")
+        for n in (4, 5):
+            tab_passes(0, n)
+        quantize_wt(3, "vector")
+        for n in (6, 7):
+            tab_passes(0, n)
+        for n in (2, 3):
+            open_tile(1, n)
+            tab_passes(1, n)
+        for n in (0, 1, 2, 3):
+            x_passes(1, n)
+        for n in (4, 5, 6, 7):
+            open_tile(1, n)
+            tab_passes(1, n)
+            x_passes(1, n)

@@ -17,13 +17,14 @@ FP4X4 = mybir.dt.float4_e2m1fn_x4
 GELU = mybir.ActivationFunctionType.Gelu_apprx_tanh
 SUB = mybir.AluOpType.subtract
 
+CFG = {'eyeV': 2, 'wq': 0, 'hold': False, 'b00': (5, 6, 7), 'x00': ('scalar', 'scalar'), 'sp01': True, 'b01': (4, 5, 6, 7), 'loads': ('g1', 'g2', 'x0', 'g3', 'x1'), 'k45': 2, 'k67': 4, 'w1': ('vector', 'vector'), 'w2': ('vector', 'vector'), 'w3': ('scalar', 'vector'), 'x10': ('vector', 'scalar'), 'x11': ('scalar', 'scalar'), 'sp10': False, 'sp11': True, 'g1': 'wt_bf2', 'bb': ((0, 1, 2), (0, 1)), 'r00': None, 'r02': None, 'r04': None, 'r06': None, 'b10': (0, 1, 2), 'b11': (0, 1), 'bank1': [3, 4, 5, 6, 7, 2, 0, 1], 'early': 6, 'res': {(0, 0): None, (0, 2): None, (0, 4): None, (0, 6): None}}
 P = 128
 PACK = 4
 K_PASS = P * PACK
 PASSES = 2
 HALF = 512
 UNIT = 256
-ACC_BANKS = 6
+WT_ENGINES = {1: ("vector", "vector"), 2: ("scalar", "vector"), 3: ("vector", "vector")}
 
 
 def interleaved(ap):
@@ -41,10 +42,12 @@ def tile_list_tiert_gelu_kernel(
     with ExitStack() as ctx:
         held = ctx.enter_context(tc.tile_pool(name="held", bufs=1))
         psum = ctx.enter_context(tc.psum_pool(name="psum", bufs=1))
-        back = ctx.enter_context(tc.psum_pool(name="back", bufs=2))
 
-        def keep(shape, dtype, name):
-            return held.tile(shape, dtype, name=name, align_bytes=64)
+        home = {}
+
+        def keep(shape, dtype, name, after=None):
+            home[name] = home[after] if after else name
+            return held.tile(shape, dtype, name=name, tag=home[name], align_bytes=64)
 
         offsets = held.tile([P, J // 16], U16, name="offsets")
         nc.sync.dma_start(offsets[:], offs)
@@ -54,53 +57,43 @@ def tile_list_tiert_gelu_kernel(
             scale_window[96:P, :].bitcast(I32),
             tab_scales.rearrange("a q t -> (a q) t").bitcast(I32),
         )
-        wx_sc = keep([P, PASSES, N], U8, "wx_sc")
-        nc.vector.memset(wx_sc[:].bitcast(I32), 0)
-        b_rows = keep([P, P], F32, "b_rows")
-        nc.vector.memset(b_rows[:], 0.0)
-        nc.vector.memset(scale_window[0:96, :].bitcast(I32), 0)
-        band = keep([P, 7 * P], F32, "band")
-        nc.vector.memset(band[:, 0 : 3 * P], 0.0)
-        nc.vector.memset(band[:, 4 * P :], 0.0)
-        make_identity(nc, band[:, 3 * P : 4 * P])
-        warm = keep([P, 8], F32, "warm")
-        nc.scalar.activation(warm[:, 0:1], band[:, 0:1], GELU)
-        for quad in range(4):
-            nc.sync.dma_start(
-                wx_sc[32 * quad : 32 * quad + 4, :, :].bitcast(I32),
-                wx_scales[:, 4 * quad : 4 * quad + 4, :].rearrange("a r n -> r a n").bitcast(I32),
-            )
-        nc.sync.dma_start(b_rows[0 : N // P, :], b.rearrange("(c p) -> c p", p=P))
-
-        def load_unit(src, a, col0, name):
-            raw = keep([P, PACK, UNIT], F32, name)
+        def load_unit(src, a, col0, name, after):
+            raw = keep([P, PACK, UNIT], F32, name, after)
             rows = src[a * K_PASS : (a + 1) * K_PASS, col0 : col0 + UNIT]
             nc.sync.dma_start(raw[:], rows.rearrange("(p t) w -> p t w", t=PACK))
             return raw
 
         x_raw, wt_raw = {}, {}
 
-        def load_x(h):
-            for a in range(PASSES):
-                for q in range(2):
-                    x_raw[h, a, q] = load_unit(x, a, h * HALF + q * UNIT, f"x_raw{h}{a}{q}")
+        def load_x(h, a, after):
+            for q in range(2):
+                x_raw[h, a, q] = load_unit(x, a, h * HALF + q * UNIT, f"x_raw{h}{a}{q}", after[q])
 
-        def load_wt(g):
+        def load_wt(g, after):
             for a in range(PASSES):
-                wt_raw[g, a] = load_unit(wt, a, g * UNIT, f"wt_raw{g}{a}")
+                wt_raw[g, a] = load_unit(wt, a, g * UNIT, f"wt_raw{g}{a}", after[a])
 
-        load_x(0)
+        b_rows = keep([P, P], F32, "b_rows")
+        nc.vector.memset(b_rows[:], 0.0)
+        load_x(0, 0, (None, None))
+        nc.sync.dma_start(b_rows[0 : N // P, :], b.rearrange("(c p) -> c p", p=P))
+        load_x(0, 1, (None, None))
+        band = keep([P, 7 * P], F32, "band")
+        nc.vector.memset(band[:], 0.0)
+        make_identity(nc, band[:, 3 * P : 4 * P], nomemset=True)
+        nc.vector.memset(scale_window[0:96, :].bitcast(I32), 0)
+        wx_sc = keep([P, PASSES, N], U8, "wx_sc")
+        nc.vector.memset(wx_sc[:].bitcast(I32), 0)
+        warm = keep([P, 8], F32, "warm")
+        nc.scalar.activation(warm[:, 0:1], band[:, 0:1], GELU)
+        for quad in range(4):
+            (nc.scalar if CFG["wq"] else nc.sync).dma_start(
+                wx_sc[32 * quad : 32 * quad + 4, :, :].bitcast(I32),
+                wx_scales[:, 4 * quad : 4 * quad + 4, :].rearrange("a r n -> r a n").bitcast(I32),
+            )
         wx_w = keep([P, PASSES, 2 * N], U8, "wx_w")
         nc.sync.dma_start(wx_w[:].bitcast(I32), wx_words.rearrange("a p c -> p a c").bitcast(I32))
-        load_wt(0)
-        word_window = keep([P, T], U32, "word_window")
-        nc.sync.dma_start(
-            word_window[:].bitcast(I32), tab_words[0].rearrange("p t c -> p (t c)").bitcast(I32)
-        )
-        load_wt(1)
-        load_x(1)
-        load_wt(2)
-        load_wt(3)
+        load_wt(0, (None, None))
 
         picked_sc = keep([P, J], U8, "picked_sc")
         nc.vector.tensor_copy(picked_sc[:], scale_window[:].indirect(offsets[:]))
@@ -110,60 +103,72 @@ def tile_list_tiert_gelu_kernel(
             nc.vector.memset(plane[:].bitcast(I32), 0)
             for quad in range(4):
                 first = 96 + 16 * a + 4 * quad
-                nc.gpsimd.dma_start(
+                nc.sync.dma_start(
                     plane[32 * quad : 32 * quad + 4, :].bitcast(I32),
                     picked_sc[first : first + 4, :].bitcast(I32),
                 )
             tab_sc.append(plane)
+            if a == 0:
+                word_window = keep([P, T], U32, "word_window", "scale_window" if CFG["hold"] else None)
+                nc.sync.dma_start(
+                    word_window[:].bitcast(I32), tab_words[0].rearrange("p t c -> p (t c)").bitcast(I32)
+                )
 
-        eye = keep([P, PACK, P, PACK], BF16, "eye")
-        for t in range(PACK):
-            copy = nc.vector.tensor_copy if t < 2 else nc.scalar.copy
-            copy(
-                interleaved(eye[:, t, :, :]),
-                planar(band[:, (3 - t) * P : (7 - t) * P].rearrange("p (t w) -> p t w", t=PACK)),
-            )
         eye_w = keep([P, PACK * P], U32, "eye_w")
         eye_sc = keep([P, PACK * P], U8, "eye_sc")
-        nc.vector.quantize_mx(eye_w[:].bitcast(FP8X4), eye_sc[:], eye[:].rearrange("p t m i -> p (t m i)"))
+        for half, copy in enumerate((nc.vector.tensor_copy if CFG["eyeV"] else nc.scalar.copy, nc.scalar.copy)):
+            eye = keep([P, 2 * P, PACK], BF16, f"eye{half}")
+            for t in (2 * half, 2 * half + 1):
+                copy(
+                    interleaved(eye[:, t % 2 * P : (t % 2 + 1) * P, :]),
+                    planar(band[:, (3 - t) * P : (7 - t) * P].rearrange("p (t w) -> p t w", t=PACK)),
+                )
+            cols = slice(2 * half * P, 2 * (half + 1) * P)
+            nc.vector.quantize_mx(eye_w[:, cols].bitcast(FP8X4), eye_sc[:, cols], eye[:].rearrange("p m i -> p (m i)"))
 
-        b_bank = back.tile([P, PACK, P], F32, name="back_bank")
+        b_bank = psum.tile([P, PACK, P], F32, name="b_bank", tag="bank0")
         nc.tensor.transpose(b_bank[:, 0, :], b_rows[:], band[:, 3 * P : 4 * P])
         bias = keep([P, N // P], F32, "bias")
         nc.scalar.copy(bias[:], b_bank[:, 0, 0 : N // P])
 
-        def cast(raw, name, engine):
-            grouped = keep([P, UNIT, PACK], BF16, name)
-            if engine == "scalar":
-                nc.scalar.copy(interleaved(grouped[:]), planar(raw[:]))
-            else:
-                nc.vector.tensor_copy(interleaved(grouped[:]), planar(raw[:]))
-            return grouped
+        def cast(grouped, raw, engine):
+            copy = nc.scalar.copy if engine == "scalar" else nc.vector.tensor_copy
+            copy(interleaved(grouped), planar(raw[:]))
 
         def quantize(grouped, words, scales):
-            nc.vector.quantize_mx(words.bitcast(FP8X4), scales, grouped[:].rearrange("p w t -> p (w t)"))
+            nc.vector.quantize_mx(words.bitcast(FP8X4), scales, grouped.rearrange("p w t -> p (w t)"))
+
+        def round_and_quantize(name, raws, engines, split, words, scales):
+            if split or engines[0] != engines[1]:
+                for u, raw in enumerate(raws):
+                    cols = slice(u * UNIT, (u + 1) * UNIT)
+                    grouped = keep([P, UNIT, PACK], BF16, name + "_first" * (1 - u))
+                    cast(grouped[:], raw, engines[u])
+                    quantize(grouped[:], words[:, cols], scales[:, cols])
+            else:
+                grouped = keep([P, 2 * UNIT, PACK], BF16, name)
+                for u, raw in enumerate(raws):
+                    cast(grouped[:, u * UNIT : (u + 1) * UNIT, :], raw, engines[u])
+                quantize(grouped[:], words[:], scales[:])
 
         xq, xr, wq = {}, {}, {}
 
-        def tier_one(h, a):
+        def tier_one(h, a, engines, split):
             words = keep([P, HALF], U32, f"xq_w{h}{a}")
             scales = keep([P, HALF], U8, f"xq_sc{h}{a}")
             xq[h, a] = (words, scales)
-            for q in range(2):
-                cols = slice(q * UNIT, (q + 1) * UNIT)
-                grouped = cast(x_raw[h, a, q], f"x_bf{h}{a}{q}", "scalar")
-                quantize(grouped, words[:, cols], scales[:, cols])
+            round_and_quantize(f"x_bf{h}{a}", [x_raw[h, a, q] for q in range(2)], engines, split, words, scales)
 
-        def tier_two(h, a):
+        def tier_two(h, a, banks):
             q_words, q_scales = xq[h, a]
             words = keep([P, HALF], U32, f"xr_w{h}{a}")
             scales = keep([P, HALF], U8, f"xr_sc{h}{a}")
             xr[h, a] = (words, scales)
+            left = keep([P, HALF, PACK], BF16, f"left{h}{a}")
             for q in range(2):
-                left = keep([P, UNIT, PACK], BF16, f"left{h}{a}{q}")
                 for s in range(UNIT // P):
                     cols = slice(q * UNIT + s * P, q * UNIT + (s + 1) * P)
-                    bank = back.tile([P, PACK, P], F32, name="back_bank")
+                    bank = psum.tile([P, PACK, P], F32, name="back", tag=f"bank{banks[(2 * q + s) % len(banks)]}")
                     for t in range(PACK):
                         nc.tensor.matmul_mx(
                             bank[:, t, :],
@@ -175,26 +180,23 @@ def tile_list_tiert_gelu_kernel(
                             stop=True,
                         )
                     nc.vector.tensor_tensor(
-                        interleaved(left[:, s * P : (s + 1) * P, :]),
+                        interleaved(left[:, cols, :]),
                         planar(x_raw[h, a, q][:, :, s * P : (s + 1) * P]),
                         planar(bank[:]),
                         SUB,
                     )
-                cols = slice(q * UNIT, (q + 1) * UNIT)
-                quantize(left, words[:, cols], scales[:, cols])
+            quantize(left[:], words[:], scales[:])
 
-        def quantize_wt(g, engine):
-            for a in range(PASSES):
-                words = keep([P, UNIT], U32, f"wt_w{g}{a}")
-                scales = keep([P, UNIT], U8, f"wt_sc{g}{a}")
-                grouped = cast(wt_raw[g, a], f"wt_bf{g}{a}", engine)
-                quantize(grouped, words[:], scales[:])
-                wq[g, a] = (words, scales)
+        def quantize_wt(g, engines):
+            words = keep([P, PASSES * UNIT], U32, f"wt_w{g}")
+            scales = keep([P, PASSES * UNIT], U8, f"wt_sc{g}")
+            round_and_quantize(f"wt_bf{g}", [wt_raw[g, a] for a in range(PASSES)], engines, False, words, scales)
+            wq[g] = (words, scales)
 
         tab_w = {}
 
-        def gather_words(h):
-            picked = keep([P, HALF], U32, f"picked_w{h}")
+        def gather_words(h, after=None):
+            picked = keep([P, HALF], U32, f"picked_w{h}", after)
             lists = offsets[:, h * HALF // 16 : (h + 1) * HALF // 16]
             nc.vector.tensor_copy(picked[:], word_window[:].indirect(lists))
             parted = keep([P, PASSES, 2 * HALF], U8, f"tab_w{h}")
@@ -203,10 +205,10 @@ def tile_list_tiert_gelu_kernel(
             )
             tab_w[h] = parted
 
-        acc, done = {}, {}
+        acc, done, results = {}, {}, {}
 
-        def open_tile(h, n):
-            acc[h, n] = psum.tile([P, HALF], F32, name=f"acc{len(acc) % ACC_BANKS}")
+        def open_tile(h, n, bank):
+            acc[h, n] = psum.tile([P, HALF], F32, name=f"acc{h}{n}", tag=f"bank{bank}")
             done[h, n] = 0
 
         def add_pass(h, n, lhsT, lhsT_scale, rhs, rhs_scale):
@@ -217,9 +219,11 @@ def tile_list_tiert_gelu_kernel(
             )
             done[h, n] = count + 1
             if count == 3 * PASSES - 1:
-                result = keep([P, HALF], F32, f"result{h}{n}")
-                nc.scalar.activation(result[:], acc[h, n][:], GELU, bias=bias[:, n : n + 1])
-                nc.sync.dma_start(out[n * P : (n + 1) * P, h * HALF : (h + 1) * HALF], result[:])
+                if n % 2 == 0:
+                    results[h, n // 2] = keep([P, 2, HALF], F32, f"result{h}{n}", CFG["res"].get((h, n)))
+                result = results[h, n // 2][:, n % 2, :]
+                nc.scalar.activation(result, acc[h, n][:], GELU, bias=bias[:, n : n + 1])
+                nc.sync.dma_start(out[n * P : (n + 1) * P, h * HALF : (h + 1) * HALF], result)
 
         def x_pass(tier, h, a, n):
             words, scales = tier[h, a]
@@ -236,52 +240,68 @@ def tile_list_tiert_gelu_kernel(
 
         def tab_passes(h, n):
             for a in range(PASSES):
-                words, scales = wq[n // 2, a]
-                cols = slice(n % 2 * P, (n % 2 + 1) * P)
+                words, scales = wq[n // 2]
+                cols = slice(a * UNIT + n % 2 * P, a * UNIT + (n % 2 + 1) * P)
                 add_pass(
                     h, n,
                     words[:, cols].bitcast(FP8X4), scales[:, cols],
                     tab_w[h][:, a, :].bitcast(FP4X4), tab_sc[a][:, h * HALF : (h + 1) * HALF],
                 )
 
-        for a in range(PASSES):
-            tier_one(0, a)
-            tier_two(0, a)
-        for n in range(ACC_BANKS):
-            open_tile(0, n)
-        for a in range(PASSES):
-            for tier in (xq, xr):
-                for n in range(ACC_BANKS):
-                    x_pass(tier, 0, a, n)
-        quantize_wt(0, "scalar")
+        tier_one(0, 0, split=True, engines=CFG["x00"])
+        tier_two(0, 0, CFG["b00"])
+        tier_one(0, 1, split=CFG["sp01"], engines=("scalar", "scalar"))
+        tier_two(0, 1, CFG["b01"])
+        holds = (("eye", "x_bf00"), ("x_raw000", "x_raw001"), ("left00", "x_bf01"), ("x_raw010", "x_raw011"), None)
+        if not CFG["hold"]:
+            holds = ((None, None),) * 5
+        later = dict(zip(CFG["loads"], holds))
+        for name in CFG["loads"][:4]:
+            if name[0] == "g":
+                load_wt(int(name[1]), later[name])
+            else:
+                load_x(1, int(name[1]), later[name])
+        quantize_wt(0, ("scalar", "scalar"))
         gather_words(0)
-        for n in (0, 1):
-            tab_passes(0, n)
-        quantize_wt(1, "scalar")
-        gather_words(1)
-        for n in (6, 7):
-            open_tile(0, n)
-            x_passes(0, n)
-        for n in (2, 3):
-            tab_passes(0, n)
-        for a in range(PASSES):
-            tier_one(1, a)
-            tier_two(1, a)
-        for n in (0, 1):
-            open_tile(1, n)
-            tab_passes(1, n)
-        quantize_wt(2, "scalar")
-        for n in (4, 5):
-            tab_passes(0, n)
-        quantize_wt(3, "vector")
-        for n in (6, 7):
-            tab_passes(0, n)
-        for n in (2, 3):
-            open_tile(1, n)
-            tab_passes(1, n)
+        name = CFG["loads"][4]
+        if name[0] == "g":
+            load_wt(int(name[1]), ("left01", "wt_bf0") if CFG["hold"] else (None, None))
+        else:
+            load_x(1, int(name[1]), ("left01", "wt_bf0") if CFG["hold"] else (None, None))
+
+        def x_sweep(h, tiles, steps):
+            for tier, a in steps:
+                for n in tiles:
+                    x_pass(tier, h, a, n)
+
+        every = ((xq, 0), (xr, 0), (xq, 1), (xr, 1))
+        for n in range(8):
+            open_tile(0, n, n)
+        x_sweep(0, range(4), every)
+        k45, k67 = CFG["k45"], CFG["k67"]
+        for step in range(4):
+            x_sweep(0, [n for n in range(4, 8) if step < (k45 if n < 6 else k67)], every[step : step + 1])
+        bank = CFG["bank1"]
+        early = CFG["early"]
+        quantize_wt(1, CFG["w1"])
+        quantize_wt(2, CFG["w2"])
+        gather_words(1, CFG["g1"])
+        quantize_wt(3, CFG["w3"])
+        tier_one(1, 0, CFG["x10"], CFG["sp10"])
+        tier_one(1, 1, CFG["x11"], CFG["sp11"])
         for n in (0, 1, 2, 3):
-            x_passes(1, n)
-        for n in (4, 5, 6, 7):
-            open_tile(1, n)
+            tab_passes(0, n)
+        for pair, k in (((4, 5), k45), ((6, 7), k67)):
+            for n in pair:
+                tab_passes(0, n)
+                x_sweep(0, (n,), every[k:])
+        tier_two(1, 0, CFG["b10"])
+        tier_two(1, 1, CFG["b11"])
+        for n in range(early):
+            open_tile(1, n, bank[n])
+            tab_passes(1, n)
+        x_sweep(1, range(early), every)
+        for n in range(early, 8):
+            open_tile(1, n, bank[n])
             tab_passes(1, n)
             x_passes(1, n)

@@ -17,14 +17,16 @@ FP4X4 = mybir.dt.float4_e2m1fn_x4
 GELU = mybir.ActivationFunctionType.Gelu_apprx_tanh
 SUB = mybir.AluOpType.subtract
 
-CFG = {'eyeV': 2, 'wq': 0, 'hold': False, 'b00': (5, 6, 7), 'x00': ('scalar', 'scalar'), 'sp01': True, 'b01': (4, 5, 6, 7), 'loads': ('g1', 'g2', 'x0', 'g3', 'x1'), 'k45': 2, 'k67': 4, 'w1': ('vector', 'vector'), 'w2': ('vector', 'vector'), 'w3': ('scalar', 'vector'), 'x10': ('vector', 'scalar'), 'x11': ('scalar', 'scalar'), 'sp10': False, 'sp11': True, 'g1': 'wt_bf2', 'bb': ((0, 1, 2), (0, 1)), 'r00': None, 'r02': None, 'r04': None, 'r06': None, 'b10': (0, 1, 2), 'b11': (0, 1), 'bank1': [3, 4, 5, 6, 7, 2, 0, 1], 'early': 6, 'res': {(0, 0): None, (0, 2): None, (0, 4): None, (0, 6): None}}
 P = 128
 PACK = 4
 K_PASS = P * PACK
 PASSES = 2
+QUADS = 4
 HALF = 512
 UNIT = 256
-WT_ENGINES = {1: ("vector", "vector"), 2: ("scalar", "vector"), 3: ("vector", "vector")}
+LIST_ROWS = 16
+SCALE_ROWS = PASSES * K_PASS // 32
+ALIGN = 256
 
 
 def interleaved(ap):
@@ -43,265 +45,232 @@ def tile_list_tiert_gelu_kernel(
         held = ctx.enter_context(tc.tile_pool(name="held", bufs=1))
         psum = ctx.enter_context(tc.psum_pool(name="psum", bufs=1))
 
-        home = {}
+        def keep(shape, dtype, name, reuse=None):
+            return held.tile(shape, dtype, name=name, tag=reuse or name, align_bytes=ALIGN)
 
-        def keep(shape, dtype, name, after=None):
-            home[name] = home[after] if after else name
-            return held.tile(shape, dtype, name=name, tag=home[name], align_bytes=64)
-
-        offsets = held.tile([P, J // 16], U16, name="offsets")
-        nc.sync.dma_start(offsets[:], offs)
-
-        scale_window = keep([P, T], U8, "scale_window")
-        nc.sync.dma_start(
-            scale_window[96:P, :].bitcast(I32),
-            tab_scales.rearrange("a q t -> (a q) t").bitcast(I32),
-        )
-        def load_unit(src, a, col0, name, after):
-            raw = keep([P, PACK, UNIT], F32, name, after)
+        def load_unit(src, a, col0, name):
+            raw = keep([P, PACK, UNIT], F32, name)
             rows = src[a * K_PASS : (a + 1) * K_PASS, col0 : col0 + UNIT]
             nc.sync.dma_start(raw[:], rows.rearrange("(p t) w -> p t w", t=PACK))
             return raw
 
-        x_raw, wt_raw = {}, {}
-
-        def load_x(h, a, after):
-            for q in range(2):
-                x_raw[h, a, q] = load_unit(x, a, h * HALF + q * UNIT, f"x_raw{h}{a}{q}", after[q])
-
-        def load_wt(g, after):
-            for a in range(PASSES):
-                wt_raw[g, a] = load_unit(wt, a, g * UNIT, f"wt_raw{g}{a}", after[a])
-
         b_rows = keep([P, P], F32, "b_rows")
         nc.vector.memset(b_rows[:], 0.0)
-        load_x(0, 0, (None, None))
-        nc.sync.dma_start(b_rows[0 : N // P, :], b.rearrange("(c p) -> c p", p=P))
-        load_x(0, 1, (None, None))
-        band = keep([P, 7 * P], F32, "band")
-        nc.vector.memset(band[:], 0.0)
-        make_identity(nc, band[:, 3 * P : 4 * P], nomemset=True)
-        nc.vector.memset(scale_window[0:96, :].bitcast(I32), 0)
         wx_sc = keep([P, PASSES, N], U8, "wx_sc")
         nc.vector.memset(wx_sc[:].bitcast(I32), 0)
-        warm = keep([P, 8], F32, "warm")
-        nc.scalar.activation(warm[:, 0:1], band[:, 0:1], GELU)
-        for quad in range(4):
-            (nc.scalar if CFG["wq"] else nc.sync).dma_start(
+        band = keep([P, (2 * PACK - 1) * P], F32, "band")
+        nc.vector.memset(band[:], 0.0)
+        identity = band[:, (PACK - 1) * P : PACK * P]
+        make_identity(nc, identity, nomemset=True)
+        scale_window = keep([P, T], U8, "scale_window")
+        first_row = P - SCALE_ROWS
+        nc.vector.memset(scale_window[0:first_row, :].bitcast(I32), 0)
+
+        offsets = held.tile([P, J // LIST_ROWS], U16, name="offsets")
+        wx_w = [keep([P, 2 * N], U8, f"wx_w{a}") for a in range(PASSES)]
+        nc.sync.dma_start(offsets[:], offs)
+        nc.sync.dma_start(
+            scale_window[first_row:P, :].bitcast(I32), tab_scales.rearrange("a q t -> (a q) t").bitcast(I32)
+        )
+        x_raw = {(h, a): [] for h in range(2) for a in range(PASSES)}
+
+        def load_x(h, a, u):
+            x_raw[h, a].append(load_unit(x, a, h * HALF + u * UNIT, f"x_raw{h}{a}{u}"))
+
+        load_x(0, 0, 0)
+        for quad in range(QUADS):
+            nc.sync.dma_start(
                 wx_sc[32 * quad : 32 * quad + 4, :, :].bitcast(I32),
                 wx_scales[:, 4 * quad : 4 * quad + 4, :].rearrange("a r n -> r a n").bitcast(I32),
             )
-        wx_w = keep([P, PASSES, 2 * N], U8, "wx_w")
-        nc.sync.dma_start(wx_w[:].bitcast(I32), wx_words.rearrange("a p c -> p a c").bitcast(I32))
-        load_wt(0, (None, None))
-
-        picked_sc = keep([P, J], U8, "picked_sc")
-        nc.vector.tensor_copy(picked_sc[:], scale_window[:].indirect(offsets[:]))
-        tab_sc = []
-        for a in range(PASSES):
-            plane = keep([P, J], U8, f"tab_sc{a}")
-            nc.vector.memset(plane[:].bitcast(I32), 0)
-            for quad in range(4):
-                first = 96 + 16 * a + 4 * quad
-                nc.sync.dma_start(
-                    plane[32 * quad : 32 * quad + 4, :].bitcast(I32),
-                    picked_sc[first : first + 4, :].bitcast(I32),
-                )
-            tab_sc.append(plane)
-            if a == 0:
-                word_window = keep([P, T], U32, "word_window", "scale_window" if CFG["hold"] else None)
-                nc.sync.dma_start(
-                    word_window[:].bitcast(I32), tab_words[0].rearrange("p t c -> p (t c)").bitcast(I32)
-                )
+        load_x(0, 0, 1)
+        nc.sync.dma_start(wx_w[0][:].bitcast(I32), wx_words[0].bitcast(I32))
+        load_x(0, 1, 0)
+        nc.sync.dma_start(b_rows[0 : N // P, :], b.rearrange("(c p) -> c p", p=P))
+        load_x(0, 1, 1)
+        nc.sync.dma_start(wx_w[1][:].bitcast(I32), wx_words[1].bitcast(I32))
 
         eye_w = keep([P, PACK * P], U32, "eye_w")
         eye_sc = keep([P, PACK * P], U8, "eye_sc")
-        for half, copy in enumerate((nc.vector.tensor_copy if CFG["eyeV"] else nc.scalar.copy, nc.scalar.copy)):
-            eye = keep([P, 2 * P, PACK], BF16, f"eye{half}")
-            for t in (2 * half, 2 * half + 1):
+        for part, copy in enumerate((nc.vector.tensor_copy, nc.scalar.copy)):
+            eye = keep([P, 2 * P, PACK], BF16, f"eye{part}")
+            for t in (2 * part, 2 * part + 1):
+                blocks = band[:, (PACK - 1 - t) * P : (2 * PACK - 1 - t) * P]
                 copy(
                     interleaved(eye[:, t % 2 * P : (t % 2 + 1) * P, :]),
-                    planar(band[:, (3 - t) * P : (7 - t) * P].rearrange("p (t w) -> p t w", t=PACK)),
+                    planar(blocks.rearrange("p (t w) -> p t w", t=PACK)),
                 )
-            cols = slice(2 * half * P, 2 * (half + 1) * P)
-            nc.vector.quantize_mx(eye_w[:, cols].bitcast(FP8X4), eye_sc[:, cols], eye[:].rearrange("p m i -> p (m i)"))
+            cols = slice(2 * part * P, 2 * (part + 1) * P)
+            nc.vector.quantize_mx(eye_w[:, cols].bitcast(FP8X4), eye_sc[:, cols], eye[:].rearrange("p m t -> p (m t)"))
 
-        b_bank = psum.tile([P, PACK, P], F32, name="b_bank", tag="bank0")
-        nc.tensor.transpose(b_bank[:, 0, :], b_rows[:], band[:, 3 * P : 4 * P])
-        bias = keep([P, N // P], F32, "bias")
-        nc.scalar.copy(bias[:], b_bank[:, 0, 0 : N // P])
-
-        def cast(grouped, raw, engine):
-            copy = nc.scalar.copy if engine == "scalar" else nc.vector.tensor_copy
-            copy(interleaved(grouped), planar(raw[:]))
+        on_scalar, on_vector = nc.scalar.copy, nc.vector.tensor_copy
 
         def quantize(grouped, words, scales):
             nc.vector.quantize_mx(words.bitcast(FP8X4), scales, grouped.rearrange("p w t -> p (w t)"))
 
-        def round_and_quantize(name, raws, engines, split, words, scales):
-            if split or engines[0] != engines[1]:
-                for u, raw in enumerate(raws):
-                    cols = slice(u * UNIT, (u + 1) * UNIT)
-                    grouped = keep([P, UNIT, PACK], BF16, name + "_first" * (1 - u))
-                    cast(grouped[:], raw, engines[u])
-                    quantize(grouped[:], words[:, cols], scales[:, cols])
-            else:
-                grouped = keep([P, 2 * UNIT, PACK], BF16, name)
-                for u, raw in enumerate(raws):
-                    cast(grouped[:, u * UNIT : (u + 1) * UNIT, :], raw, engines[u])
-                quantize(grouped[:], words[:], scales[:])
+        def round_and_quantize(name, units, copies, one_stage=False):
+            words = keep([P, 2 * UNIT], U32, name + "_w")
+            scales = keep([P, 2 * UNIT], U8, name + "_sc")
+            for u in range(2):
+                cols = slice(u * UNIT, (u + 1) * UNIT)
+                grouped = keep([P, UNIT, PACK], BF16, f"{name}_bf{u}", f"{name}_bf0" if one_stage else None)
+                copies[u](interleaved(grouped[:]), planar(units[u][:]))
+                quantize(grouped[:], words[:, cols], scales[:, cols])
+            return words, scales
 
-        xq, xr, wq = {}, {}, {}
+        xq, xr, wq, tab_w = {}, {}, {}, {}
 
-        def tier_one(h, a, engines, split):
-            words = keep([P, HALF], U32, f"xq_w{h}{a}")
-            scales = keep([P, HALF], U8, f"xq_sc{h}{a}")
-            xq[h, a] = (words, scales)
-            round_and_quantize(f"x_bf{h}{a}", [x_raw[h, a, q] for q in range(2)], engines, split, words, scales)
+        def tier_one(h, a, copies, one_stage=False):
+            xq[h, a] = round_and_quantize(f"xq{h}{a}", x_raw[h, a], copies, one_stage)
 
-        def tier_two(h, a, banks):
+        def tier_two(h, a, banks, reuse=None):
             q_words, q_scales = xq[h, a]
             words = keep([P, HALF], U32, f"xr_w{h}{a}")
             scales = keep([P, HALF], U8, f"xr_sc{h}{a}")
             xr[h, a] = (words, scales)
-            left = keep([P, HALF, PACK], BF16, f"left{h}{a}")
-            for q in range(2):
-                for s in range(UNIT // P):
-                    cols = slice(q * UNIT + s * P, q * UNIT + (s + 1) * P)
-                    bank = psum.tile([P, PACK, P], F32, name="back", tag=f"bank{banks[(2 * q + s) % len(banks)]}")
-                    for t in range(PACK):
-                        nc.tensor.matmul_mx(
-                            bank[:, t, :],
-                            lhsT=eye_w[:, t * P : (t + 1) * P].bitcast(FP8X4),
-                            lhsT_scale=eye_sc[:, t * P : (t + 1) * P],
-                            rhs=q_words[:, cols].bitcast(FP8X4),
-                            rhs_scale=q_scales[:, cols],
-                            start=True,
-                            stop=True,
-                        )
-                    nc.vector.tensor_tensor(
-                        interleaved(left[:, cols, :]),
-                        planar(x_raw[h, a, q][:, :, s * P : (s + 1) * P]),
-                        planar(bank[:]),
-                        SUB,
+            left = keep([P, HALF, PACK], BF16, f"left{h}{a}", reuse)
+            for s in range(HALF // P):
+                cols = slice(s * P, (s + 1) * P)
+                back = psum.tile([P, PACK, P], F32, name="back", tag=f"bank{banks[s % len(banks)]}")
+                for t in range(PACK):
+                    nc.tensor.matmul_mx(
+                        back[:, t, :],
+                        lhsT=eye_w[:, t * P : (t + 1) * P].bitcast(FP8X4),
+                        lhsT_scale=eye_sc[:, t * P : (t + 1) * P],
+                        rhs=q_words[:, cols].bitcast(FP8X4),
+                        rhs_scale=q_scales[:, cols],
+                        start=True,
+                        stop=True,
                     )
+                unit, within = divmod(s * P, UNIT)
+                nc.vector.tensor_tensor(
+                    interleaved(left[:, cols, :]),
+                    planar(x_raw[h, a][unit][:, :, within : within + P]),
+                    planar(back[:]),
+                    SUB,
+                )
             quantize(left[:], words[:], scales[:])
 
-        def quantize_wt(g, engines):
-            words = keep([P, PASSES * UNIT], U32, f"wt_w{g}")
-            scales = keep([P, PASSES * UNIT], U8, f"wt_sc{g}")
-            round_and_quantize(f"wt_bf{g}", [wt_raw[g, a] for a in range(PASSES)], engines, False, words, scales)
-            wq[g] = (words, scales)
+        def quantize_wt(pair, copies, one_stage=False):
+            words, scales = round_and_quantize(f"wq{pair}", wt_raw[pair], copies, one_stage)
+            for n in (2 * pair, 2 * pair + 1):
+                for a in range(PASSES):
+                    cols = slice(a * UNIT + n % 2 * P, a * UNIT + (n % 2 + 1) * P)
+                    wq[n, a] = (words[:, cols], scales[:, cols])
 
-        tab_w = {}
-
-        def gather_words(h, after=None):
-            picked = keep([P, HALF], U32, f"picked_w{h}", after)
-            lists = offsets[:, h * HALF // 16 : (h + 1) * HALF // 16]
-            nc.vector.tensor_copy(picked[:], word_window[:].indirect(lists))
-            parted = keep([P, PASSES, 2 * HALF], U8, f"tab_w{h}")
+        def gather_words(h):
+            picked = keep([P, HALF], U32, f"picked_w{h}")
+            entries = offsets[:, h * HALF // LIST_ROWS : (h + 1) * HALF // LIST_ROWS]
+            nc.vector.tensor_copy(picked[:], word_window[:].indirect(entries))
+            tab_w[h] = keep([P, PASSES, 2 * HALF], U8, f"tab_w{h}")
             nc.vector.tensor_copy(
-                parted[:].bitcast(U16), picked[:].bitcast(U16).rearrange("p (j d) -> p d j", d=PASSES)
+                tab_w[h][:].bitcast(U16), picked[:].bitcast(U16).rearrange("p (j a) -> p a j", a=PASSES)
             )
-            tab_w[h] = parted
 
-        acc, done, results = {}, {}, {}
+        picked_sc = keep([P, J], U8, "picked_sc")
+        nc.vector.tensor_copy(picked_sc[:], scale_window[:].indirect(offsets[:]))
+        bias = keep([P, N // P], F32, "bias")
 
-        def open_tile(h, n, bank):
-            acc[h, n] = psum.tile([P, HALF], F32, name=f"acc{h}{n}", tag=f"bank{bank}")
-            done[h, n] = 0
+        acc, done = {}, {}
 
         def add_pass(h, n, lhsT, lhsT_scale, rhs, rhs_scale):
-            count = done[h, n]
+            count = done.get((h, n), 0)
+            last = count == 3 * PASSES - 1
+            if count == 0:
+                acc[h, n] = psum.tile([P, HALF], F32, name=f"acc{h}{n}", tag=f"bank{n}")
             nc.tensor.matmul_mx(
                 acc[h, n][:], lhsT=lhsT, lhsT_scale=lhsT_scale, rhs=rhs, rhs_scale=rhs_scale,
-                start=count == 0, stop=count == 3 * PASSES - 1,
+                start=count == 0, stop=last,
             )
             done[h, n] = count + 1
-            if count == 3 * PASSES - 1:
-                if n % 2 == 0:
-                    results[h, n // 2] = keep([P, 2, HALF], F32, f"result{h}{n}", CFG["res"].get((h, n)))
-                result = results[h, n // 2][:, n % 2, :]
-                nc.scalar.activation(result, acc[h, n][:], GELU, bias=bias[:, n : n + 1])
-                nc.sync.dma_start(out[n * P : (n + 1) * P, h * HALF : (h + 1) * HALF], result)
+            if last:
+                result = keep([P, HALF], F32, f"result{h}{n}")
+                nc.scalar.activation(result[:], acc[h, n][:], GELU, bias=bias[:, n : n + 1])
+                nc.sync.dma_start(out[n * P : (n + 1) * P, h * HALF : (h + 1) * HALF], result[:])
 
-        def x_pass(tier, h, a, n):
-            words, scales = tier[h, a]
-            add_pass(
-                h, n,
-                wx_w[:, a, 2 * n * P : 2 * (n + 1) * P].bitcast(FP4X4), wx_sc[:, a, n * P : (n + 1) * P],
-                words[:].bitcast(FP8X4), scales[:],
-            )
+        def x_passes(h, tiles, steps):
+            for tier, a in steps:
+                words, scales = tier[h, a]
+                for n in tiles:
+                    add_pass(
+                        h, n,
+                        wx_w[a][:, 2 * n * P : 2 * (n + 1) * P].bitcast(FP4X4), wx_sc[:, a, n * P : (n + 1) * P],
+                        words[:].bitcast(FP8X4), scales[:],
+                    )
 
-        def x_passes(h, n):
+        def tab_passes(h, tiles):
             for a in range(PASSES):
-                x_pass(xq, h, a, n)
-                x_pass(xr, h, a, n)
+                for n in tiles:
+                    words, scales = wq[n, a]
+                    add_pass(
+                        h, n,
+                        words.bitcast(FP8X4), scales,
+                        tab_w[h][:, a, :].bitcast(FP4X4), tab_sc[a][:, h * HALF : (h + 1) * HALF],
+                    )
 
-        def tab_passes(h, n):
-            for a in range(PASSES):
-                words, scales = wq[n // 2]
-                cols = slice(a * UNIT + n % 2 * P, a * UNIT + (n % 2 + 1) * P)
-                add_pass(
-                    h, n,
-                    words[:, cols].bitcast(FP8X4), scales[:, cols],
-                    tab_w[h][:, a, :].bitcast(FP4X4), tab_sc[a][:, h * HALF : (h + 1) * HALF],
+        every_x = ((xq, 0), (xr, 0), (xq, 1), (xr, 1))
+        pairs = [(2 * pair, 2 * pair + 1) for pair in range(N // UNIT)]
+
+        early = pairs[0] + pairs[1] + pairs[2]
+        tier_one(0, 0, (on_scalar, on_scalar))
+        tier_two(0, 0, pairs[2] + pairs[3], reuse="xq00_bf1")
+        x_passes(0, early, every_x[:1])
+        tier_one(0, 1, (on_scalar, on_scalar))
+        tier_two(0, 1, pairs[3])
+
+        b_bank = psum.tile([P, PACK, P], F32, name="b_bank", tag=f"bank{pairs[3][1]}")
+        nc.tensor.transpose(b_bank[:, 0, :], b_rows[:], identity)
+        nc.scalar.copy(bias[:], b_bank[:, 0, 0 : N // P])
+
+        tab_sc = [keep([P, J], U8, f"tab_sc{a}") for a in range(PASSES)]
+        for a in range(PASSES):
+            nc.vector.memset(tab_sc[a][:].bitcast(I32), 0)
+        word_window = keep([P, T], U32, "word_window")
+        for a in range(PASSES):
+            for quad in range(QUADS):
+                row = first_row + 4 * (QUADS * a + quad)
+                nc.gpsimd.dma_start(
+                    tab_sc[a][32 * quad : 32 * quad + 4, :].bitcast(I32), picked_sc[row : row + 4, :].bitcast(I32)
                 )
 
-        tier_one(0, 0, split=True, engines=CFG["x00"])
-        tier_two(0, 0, CFG["b00"])
-        tier_one(0, 1, split=CFG["sp01"], engines=("scalar", "scalar"))
-        tier_two(0, 1, CFG["b01"])
-        holds = (("eye", "x_bf00"), ("x_raw000", "x_raw001"), ("left00", "x_bf01"), ("x_raw010", "x_raw011"), None)
-        if not CFG["hold"]:
-            holds = ((None, None),) * 5
-        later = dict(zip(CFG["loads"], holds))
-        for name in CFG["loads"][:4]:
-            if name[0] == "g":
-                load_wt(int(name[1]), later[name])
-            else:
-                load_x(1, int(name[1]), later[name])
-        quantize_wt(0, ("scalar", "scalar"))
+        wt_raw = {}
+
+        def load_wt(pair):
+            wt_raw[pair] = [load_unit(wt, a, pair * UNIT, f"wt_raw{pair}{a}") for a in range(PASSES)]
+
+        load_wt(0)
+        nc.sync.dma_start(word_window[:].bitcast(I32), tab_words[0].rearrange("p t c -> p (t c)").bitcast(I32))
+        load_wt(1)
+        load_wt(2)
+        load_x(1, 0, 0)
+        load_x(1, 0, 1)
+        load_wt(3)
+        load_x(1, 1, 0)
+        load_x(1, 1, 1)
+
+        x_passes(0, early, every_x[1:])
+        x_passes(0, pairs[3], every_x)
         gather_words(0)
-        name = CFG["loads"][4]
-        if name[0] == "g":
-            load_wt(int(name[1]), ("left01", "wt_bf0") if CFG["hold"] else (None, None))
-        else:
-            load_x(1, int(name[1]), ("left01", "wt_bf0") if CFG["hold"] else (None, None))
+        gather_words(1)
 
-        def x_sweep(h, tiles, steps):
-            for tier, a in steps:
-                for n in tiles:
-                    x_pass(tier, h, a, n)
-
-        every = ((xq, 0), (xr, 0), (xq, 1), (xr, 1))
-        for n in range(8):
-            open_tile(0, n, n)
-        x_sweep(0, range(4), every)
-        k45, k67 = CFG["k45"], CFG["k67"]
-        for step in range(4):
-            x_sweep(0, [n for n in range(4, 8) if step < (k45 if n < 6 else k67)], every[step : step + 1])
-        bank = CFG["bank1"]
-        early = CFG["early"]
-        quantize_wt(1, CFG["w1"])
-        quantize_wt(2, CFG["w2"])
-        gather_words(1, CFG["g1"])
-        quantize_wt(3, CFG["w3"])
-        tier_one(1, 0, CFG["x10"], CFG["sp10"])
-        tier_one(1, 1, CFG["x11"], CFG["sp11"])
-        for n in (0, 1, 2, 3):
-            tab_passes(0, n)
-        for pair, k in (((4, 5), k45), ((6, 7), k67)):
-            for n in pair:
-                tab_passes(0, n)
-                x_sweep(0, (n,), every[k:])
-        tier_two(1, 0, CFG["b10"])
-        tier_two(1, 1, CFG["b11"])
-        for n in range(early):
-            open_tile(1, n, bank[n])
-            tab_passes(1, n)
-        x_sweep(1, range(early), every)
-        for n in range(early, 8):
-            open_tile(1, n, bank[n])
-            tab_passes(1, n)
-            x_passes(1, n)
+        quantize_wt(0, (on_scalar, on_scalar))
+        quantize_wt(1, (on_scalar, on_scalar))
+        tab_passes(0, pairs[0])
+        tab_passes(0, pairs[1])
+        quantize_wt(2, (on_vector, on_vector), one_stage=True)
+        tab_passes(1, pairs[0])
+        tab_passes(0, pairs[2])
+        tier_one(1, 0, (on_vector, on_vector), one_stage=True)
+        quantize_wt(3, (on_scalar, on_scalar))
+        tier_one(1, 1, (on_scalar, on_vector))
+        tier_two(1, 0, pairs[1])
+        tab_passes(0, pairs[3])
+        tab_passes(1, pairs[2])
+        x_passes(1, pairs[0] + pairs[2], every_x[:1])
+        tier_two(1, 1, pairs[1])
+        tab_passes(1, pairs[3])
+        x_passes(1, pairs[3], every_x[:1])
+        x_passes(1, pairs[0] + pairs[2] + pairs[3], every_x[1:])
+        for n in pairs[1]:
+            tab_passes(1, (n,))
+            x_passes(1, (n,), every_x)

@@ -226,12 +226,15 @@ def tile_list_tiert_gelu_kernel(
         for a in range(PASSES):
             nc.vector.memset(tab_sc[a][:].bitcast(I32), 0)
         word_window = keep([P, T], U32, "word_window")
-        for a in range(PASSES):
+
+        def move_scales(a, queue):
             for quad in range(QUADS):
                 row = first_row + 4 * (QUADS * a + quad)
-                nc.gpsimd.dma_start(
+                queue.dma_start(
                     tab_sc[a][32 * quad : 32 * quad + 4, :].bitcast(I32), picked_sc[row : row + 4, :].bitcast(I32)
                 )
+
+        move_scales(0, nc.gpsimd)
 
         wt_raw = {}
 
@@ -241,6 +244,7 @@ def tile_list_tiert_gelu_kernel(
         load_wt(0)
         nc.sync.dma_start(word_window[:].bitcast(I32), tab_words[0].rearrange("p t c -> p (t c)").bitcast(I32))
         load_wt(1)
+        move_scales(1, nc.sync)
         load_wt(2)
         load_x(1, 0, 0)
         load_x(1, 0, 1)

@@ -1,7 +1,6 @@
 from contextlib import ExitStack
 
 import concourse.mybir as mybir
-from concourse.masks import make_identity
 
 K, L, N, T, J = 1024, 1024, 1024, 4096, 1024
 FLOPS = 2 * N * J * (K + 2 * L) + 2 * 512 * L * J
@@ -16,6 +15,7 @@ FP8X4 = mybir.dt.float8_e4m3fn_x4
 FP4X4 = mybir.dt.float4_e2m1fn_x4
 GELU = mybir.ActivationFunctionType.Gelu_apprx_tanh
 SUB = mybir.AluOpType.subtract
+ADD = mybir.AluOpType.add
 
 P = 128
 PACK = 4
@@ -26,6 +26,7 @@ HALF = 512
 UNIT = 256
 LIST_ROWS = 16
 SCALE_ROWS = PASSES * K_PASS // 32
+LEAD = 32
 ALIGN = 256
 
 
@@ -44,84 +45,92 @@ def tile_list_tiert_gelu_kernel(
     with ExitStack() as ctx:
         held = ctx.enter_context(tc.tile_pool(name="held", bufs=1))
         psum = ctx.enter_context(tc.psum_pool(name="psum", bufs=1))
+        on_scalar, on_vector = nc.scalar.copy, nc.vector.tensor_copy
 
         def keep(shape, dtype, name, reuse=None):
             return held.tile(shape, dtype, name=name, tag=reuse or name, align_bytes=ALIGN)
 
-        def load_unit(src, a, col0, name):
-            raw = keep([P, PACK, UNIT], F32, name)
-            rows = src[a * K_PASS : (a + 1) * K_PASS, col0 : col0 + UNIT]
+        def load_rows(src, a, col0, width, name):
+            raw = keep([P, PACK, width], F32, name)
+            rows = src[a * K_PASS : (a + 1) * K_PASS, col0 : col0 + width]
             nc.sync.dma_start(raw[:], rows.rearrange("(p t) w -> p t w", t=PACK))
             return raw
-
-        b_rows = keep([P, P], F32, "b_rows")
-        nc.vector.memset(b_rows[:], 0.0)
-        wx_sc = keep([P, PASSES, N], U8, "wx_sc")
-        nc.vector.memset(wx_sc[:].bitcast(I32), 0)
-        band = keep([P, (2 * PACK - 1) * P], F32, "band")
-        nc.vector.memset(band[:], 0.0)
-        identity = band[:, (PACK - 1) * P : PACK * P]
-        make_identity(nc, identity, nomemset=True)
-        scale_window = keep([P, T], U8, "scale_window")
-        first_row = P - SCALE_ROWS
-        nc.vector.memset(scale_window[0:first_row, :].bitcast(I32), 0)
-
-        offsets = held.tile([P, J // LIST_ROWS], U16, name="offsets")
-        wx_w = [keep([P, 2 * N], U8, f"wx_w{a}") for a in range(PASSES)]
-        nc.sync.dma_start(offsets[:], offs)
-        nc.sync.dma_start(
-            scale_window[first_row:P, :].bitcast(I32), tab_scales.rearrange("a q t -> (a q) t").bitcast(I32)
-        )
-        x_raw = {(h, a): [] for h in range(2) for a in range(PASSES)}
-
-        def load_x(h, a, u):
-            x_raw[h, a].append(load_unit(x, a, h * HALF + u * UNIT, f"x_raw{h}{a}{u}"))
-
-        load_x(0, 0, 0)
-        for quad in range(QUADS):
-            nc.sync.dma_start(
-                wx_sc[32 * quad : 32 * quad + 4, :, :].bitcast(I32),
-                wx_scales[:, 4 * quad : 4 * quad + 4, :].rearrange("a r n -> r a n").bitcast(I32),
-            )
-        load_x(0, 0, 1)
-        nc.sync.dma_start(wx_w[0][:].bitcast(I32), wx_words[0].bitcast(I32))
-        load_x(0, 1, 0)
-        nc.sync.dma_start(b_rows[0 : N // P, :], b.rearrange("(c p) -> c p", p=P))
-        load_x(0, 1, 1)
-        nc.sync.dma_start(wx_w[1][:].bitcast(I32), wx_words[1].bitcast(I32))
-
-        eye_w = keep([P, PACK * P], U32, "eye_w")
-        eye_sc = keep([P, PACK * P], U8, "eye_sc")
-        for part, copy in enumerate((nc.vector.tensor_copy, nc.scalar.copy)):
-            eye = keep([P, 2 * P, PACK], BF16, f"eye{part}")
-            for t in (2 * part, 2 * part + 1):
-                blocks = band[:, (PACK - 1 - t) * P : (2 * PACK - 1 - t) * P]
-                copy(
-                    interleaved(eye[:, t % 2 * P : (t % 2 + 1) * P, :]),
-                    planar(blocks.rearrange("p (t w) -> p t w", t=PACK)),
-                )
-            cols = slice(2 * part * P, 2 * (part + 1) * P)
-            nc.vector.quantize_mx(eye_w[:, cols].bitcast(FP8X4), eye_sc[:, cols], eye[:].rearrange("p m t -> p (m t)"))
-
-        on_scalar, on_vector = nc.scalar.copy, nc.vector.tensor_copy
 
         def quantize(grouped, words, scales):
             nc.vector.quantize_mx(words.bitcast(FP8X4), scales, grouped.rearrange("p w t -> p (w t)"))
 
-        def round_and_quantize(name, units, copies, one_stage=False):
-            words = keep([P, 2 * UNIT], U32, name + "_w")
-            scales = keep([P, 2 * UNIT], U8, name + "_sc")
-            for u in range(2):
-                cols = slice(u * UNIT, (u + 1) * UNIT)
-                grouped = keep([P, UNIT, PACK], BF16, f"{name}_bf{u}", f"{name}_bf0" if one_stage else None)
-                copies[u](interleaved(grouped[:]), planar(units[u][:]))
-                quantize(grouped[:], words[:, cols], scales[:, cols])
-            return words, scales
-
+        offsets = held.tile([P, J // LIST_ROWS], U16, name="offsets")
+        wx_w = [keep([P, 2 * N], U8, f"wx_w{a}") for a in range(PASSES)]
+        wx_sc = keep([P, PASSES, N], U8, "wx_sc")
+        scale_window = keep([P, T], U8, "scale_window")
+        word_window = keep([P, T], U32, "word_window")
+        picked_sc = keep([P, J], U8, "picked_sc")
+        tab_sc = [keep([P, J], U8, f"tab_sc{a}") for a in range(PASSES)]
+        bias = keep([P, N // P], F32, "bias")
+        eye_w = keep([P, PACK * P], U32, "eye_w")
+        eye_sc = keep([P, PACK * P], U8, "eye_sc")
+        first_row = P - SCALE_ROWS
+        x_raw, wt_raw = {}, {}
         xq, xr, wq, tab_w = {}, {}, {}, {}
+        acc, done = {}, {}
 
-        def tier_one(h, a, copies, one_stage=False):
-            xq[h, a] = round_and_quantize(f"xq{h}{a}", x_raw[h, a], copies, one_stage)
+        def load_x(h, a, col0, width):
+            raw = load_rows(x, a, h * HALF + col0, width, f"x_raw{h}{a}{col0 // P}")
+            for s in range(width // P):
+                x_raw[h, a, col0 // P + s] = raw[:, :, s * P : (s + 1) * P]
+            x_raw[h, a, col0, width] = raw
+
+        def load_wt(a, n0, tiles):
+            wt_raw[a, n0] = load_rows(wt, a, n0 * P, tiles * P, f"wt_raw{a}{n0}")
+
+        def load_wx(a):
+            nc.sync.dma_start(wx_w[a][:].bitcast(I32), wx_words[a].bitcast(I32))
+
+        def load_wx_scales(queue):
+            for r in range(4):
+                queue.dma_start(
+                    wx_sc[r:P:32, :, :].bitcast(I32),
+                    wx_scales[:, r:16:4, :].rearrange("a q n -> q a n").bitcast(I32),
+                )
+
+        def load_tab_scales():
+            nc.sync.dma_start(
+                scale_window[first_row:P, :].bitcast(I32), tab_scales.rearrange("a q t -> (a q) t").bitcast(I32)
+            )
+
+        def load_table():
+            nc.sync.dma_start(word_window[:].bitcast(I32), tab_words[0].rearrange("p t c -> p (t c)").bitcast(I32))
+
+        def move_scales(a, queue):
+            for r in range(4):
+                row = first_row + 16 * a + r
+                queue.dma_start(
+                    tab_sc[a][r:P:32, :].bitcast(I32), picked_sc[row : row + 13 : 4, :].bitcast(I32)
+                )
+
+        def make_eye():
+            eye = keep([P, LEAD + PACK * K_PASS], BF16, "eye")
+            two = 2 * K_PASS
+            nc.gpsimd.memset(eye[:, 0 : LEAD + two].bitcast(I32), 0)
+            low = eye[:, LEAD : LEAD + two].rearrange("p (t f) -> p t f", t=2)
+            nc.gpsimd.affine_select(
+                out=low, in_=low, compare_op=mybir.AluOpType.not_equal, fill=1.0,
+                base=0, pattern=[[-1, 2], [1, K_PASS]], channel_multiplier=-PACK,
+            )
+            nc.vector.tensor_copy(eye[:, LEAD + two :], eye[:, LEAD - 2 : LEAD - 2 + two])
+            nc.vector.quantize_mx(eye_w[:].bitcast(FP8X4), eye_sc[:], eye[:, LEAD:])
+
+        def round_cols(raw, grouped, shares):
+            for copy, c0, c1 in shares:
+                copy(interleaved(grouped[:, c0:c1, :]), planar(raw[:, :, c0:c1]))
+
+        def tier_one(h, a, col0, width, raw, off, shares, reuse=None):
+            if (h, a) not in xq:
+                xq[h, a] = (keep([P, HALF], U32, f"xq_w{h}{a}"), keep([P, HALF], U8, f"xq_sc{h}{a}"))
+            words, scales = xq[h, a]
+            grouped = keep([P, width, PACK], BF16, f"xq_bf{h}{a}{col0 // P}", reuse)
+            round_cols(raw[:, :, off : off + width], grouped, shares)
+            quantize(grouped[:], words[:, col0 : col0 + width], scales[:, col0 : col0 + width])
 
         def tier_two(h, a, banks, reuse=None):
             q_words, q_scales = xq[h, a]
@@ -142,24 +151,23 @@ def tile_list_tiert_gelu_kernel(
                         start=True,
                         stop=True,
                     )
-                unit, within = divmod(s * P, UNIT)
-                nc.vector.tensor_tensor(
-                    interleaved(left[:, cols, :]),
-                    planar(x_raw[h, a][unit][:, :, within : within + P]),
-                    planar(back[:]),
-                    SUB,
-                )
+                nc.vector.tensor_tensor(interleaved(left[:, cols, :]), planar(x_raw[h, a, s]), planar(back[:]), SUB)
             quantize(left[:], words[:], scales[:])
 
-        def quantize_wt(pair, copies, one_stage=False):
-            words, scales = round_and_quantize(f"wq{pair}", wt_raw[pair], copies, one_stage)
-            for n in (2 * pair, 2 * pair + 1):
-                for a in range(PASSES):
-                    cols = slice(a * UNIT + n % 2 * P, a * UNIT + (n % 2 + 1) * P)
-                    wq[n, a] = (words[:, cols], scales[:, cols])
+        def quantize_wt(a, n0, off, tiles, shares, reuse=None):
+            name = f"wq{a}{n0 + off}"
+            words, scales = keep([P, tiles * P], U32, name + "_w"), keep([P, tiles * P], U8, name + "_sc")
+            grouped = keep([P, tiles * P, PACK], BF16, name + "_bf", reuse)
+            round_cols(wt_raw[a, n0][:, :, off * P : (off + tiles) * P], grouped, shares)
+            quantize(grouped[:], words[:], scales[:])
+            for i in range(tiles):
+                wq[n0 + off + i, a] = (words[:, i * P : (i + 1) * P], scales[:, i * P : (i + 1) * P])
+
+        def gather_scales():
+            nc.vector.tensor_copy(picked_sc[:], scale_window[:].indirect(offsets[:]))
 
         def gather_words(h):
-            picked = keep([P, HALF], U32, f"picked_w{h}")
+            picked = keep([P, HALF], U32, f"picked_w{h}", "picked_w0")
             entries = offsets[:, h * HALF // LIST_ROWS : (h + 1) * HALF // LIST_ROWS]
             nc.vector.tensor_copy(picked[:], word_window[:].indirect(entries))
             tab_w[h] = keep([P, PASSES, 2 * HALF], U8, f"tab_w{h}")
@@ -167,114 +175,130 @@ def tile_list_tiert_gelu_kernel(
                 tab_w[h][:].bitcast(U16), picked[:].bitcast(U16).rearrange("p (j a) -> p a j", a=PASSES)
             )
 
-        picked_sc = keep([P, J], U8, "picked_sc")
-        nc.vector.tensor_copy(picked_sc[:], scale_window[:].indirect(offsets[:]))
-        bias = keep([P, N // P], F32, "bias")
-
-        acc, done = {}, {}
-
-        def add_pass(h, n, lhsT, lhsT_scale, rhs, rhs_scale):
+        def add_pass(h, n, bank, lhsT, lhsT_scale, rhs, rhs_scale):
             count = done.get((h, n), 0)
+            split = (h, n) in parked
+            first = count == 0 or (split and count == 2 * PASSES)
             last = count == 3 * PASSES - 1
-            if count == 0:
-                acc[h, n] = psum.tile([P, HALF], F32, name=f"acc{h}{n}", tag=f"bank{n}")
+            park = split and count == 2 * PASSES - 1
+            if first:
+                acc[h, n] = psum.tile([P, HALF], F32, name=f"acc{h}{n}", tag=f"bank{bank}")
             nc.tensor.matmul_mx(
                 acc[h, n][:], lhsT=lhsT, lhsT_scale=lhsT_scale, rhs=rhs, rhs_scale=rhs_scale,
-                start=count == 0, stop=last,
+                start=first, stop=last or park,
             )
             done[h, n] = count + 1
+            if park:
+                parked[h, n] = keep([P, HALF], F32, f"parked{h}{n}")
+                nc.scalar.copy(parked[h, n][:], acc[h, n][:])
             if last:
-                result = keep([P, HALF], F32, f"result{h}{n}")
-                nc.scalar.activation(result[:], acc[h, n][:], GELU, bias=bias[:, n : n + 1])
+                total = acc[h, n]
+                if split:
+                    total = parked[h, n]
+                    nc.vector.tensor_tensor(total[:], total[:], acc[h, n][:], ADD)
+                result = keep([P, HALF], F32, f"result{h}{n}", spare.pop() if spare else None)
+                nc.scalar.activation(result[:], total[:], GELU, bias=bias[:, n : n + 1])
                 nc.sync.dma_start(out[n * P : (n + 1) * P, h * HALF : (h + 1) * HALF], result[:])
 
-        def x_passes(h, tiles, steps):
+        parked = {}
+        spare = [f"xq_bf{h}{a}{s}" for h in (1, 0) for a in (1, 0) for s in (2, 0)]
+        bank_of = {}
+
+        def x_passes(tiles, steps):
             for tier, a in steps:
-                words, scales = tier[h, a]
-                for n in tiles:
+                for h, n in tiles:
+                    words, scales = tier[h, a]
                     add_pass(
-                        h, n,
+                        h, n, bank_of[h, n],
                         wx_w[a][:, 2 * n * P : 2 * (n + 1) * P].bitcast(FP4X4), wx_sc[:, a, n * P : (n + 1) * P],
                         words[:].bitcast(FP8X4), scales[:],
                     )
 
-        def tab_passes(h, tiles):
-            for a in range(PASSES):
-                for n in tiles:
+        def tab_passes(tiles, passes=(0, 1)):
+            for a in passes:
+                for h, n in tiles:
                     words, scales = wq[n, a]
                     add_pass(
-                        h, n,
+                        h, n, bank_of[h, n],
                         words.bitcast(FP8X4), scales,
                         tab_w[h][:, a, :].bitcast(FP4X4), tab_sc[a][:, h * HALF : (h + 1) * HALF],
                     )
 
         every_x = ((xq, 0), (xr, 0), (xq, 1), (xr, 1))
-        pairs = [(2 * pair, 2 * pair + 1) for pair in range(N // UNIT)]
+        S, V = on_scalar, on_vector
 
-        early = pairs[0] + pairs[1] + pairs[2]
-        tier_one(0, 0, (on_scalar, on_scalar))
-        tier_two(0, 0, pairs[2] + pairs[3], reuse="xq00_bf1")
-        x_passes(0, early, every_x[:1])
-        tier_one(0, 1, (on_scalar, on_scalar))
-        tier_two(0, 1, pairs[3])
-
-        b_bank = psum.tile([P, PACK, P], F32, name="b_bank", tag=f"bank{pairs[3][1]}")
-        nc.tensor.transpose(b_bank[:, 0, :], b_rows[:], identity)
-        nc.scalar.copy(bias[:], b_bank[:, 0, 0 : N // P])
-
-        tab_sc = [keep([P, J], U8, f"tab_sc{a}") for a in range(PASSES)]
+        nc.vector.memset(wx_sc[:].bitcast(I32), 0)
+        nc.vector.memset(scale_window[0:first_row, :].bitcast(I32), 0)
+        make_eye()
+        nc.sync.dma_start(offsets[:], offs)
+        load_tab_scales()
+        load_x(0, 0, 0, 256)
+        load_x(0, 0, 256, 256)
+        load_wx(0)
+        load_wx_scales(nc.sync)
+        load_x(0, 1, 0, 512)
+        load_wx(1)
+        load_x(1, 0, 0, 512)
+        load_x(1, 1, 0, 512)
+        gather_scales()
         for a in range(PASSES):
             nc.vector.memset(tab_sc[a][:].bitcast(I32), 0)
-        word_window = keep([P, T], U32, "word_window")
-
-        def move_scales(a, queue):
-            for quad in range(QUADS):
-                row = first_row + 4 * (QUADS * a + quad)
-                queue.dma_start(
-                    tab_sc[a][32 * quad : 32 * quad + 4, :].bitcast(I32), picked_sc[row : row + 4, :].bitcast(I32)
-                )
-
+        with nc.allow_non_contiguous_dma(reason="one bias value a partition and tile"):
+            nc.sync.dma_start(bias[:], b.rearrange("(c p) -> p c", p=P))
+        load_table()
+        load_wt(0, 0, 2)
         move_scales(0, nc.gpsimd)
-
-        wt_raw = {}
-
-        def load_wt(pair):
-            wt_raw[pair] = [load_unit(wt, a, pair * UNIT, f"wt_raw{pair}{a}") for a in range(PASSES)]
-
-        load_wt(0)
-        nc.sync.dma_start(word_window[:].bitcast(I32), tab_words[0].rearrange("p t c -> p (t c)").bitcast(I32))
-        load_wt(1)
-        move_scales(1, nc.sync)
-        load_wt(2)
-        load_x(1, 0, 0)
-        load_x(1, 0, 1)
-        load_wt(3)
-        load_x(1, 1, 0)
-        load_x(1, 1, 1)
-
-        x_passes(0, early, every_x[1:])
-        x_passes(0, pairs[3], every_x)
+        load_wt(1, 0, 2)
+        move_scales(1, nc.gpsimd)
+        for n0 in (2, 4, 6):
+            load_wt(0, n0, 2)
+            load_wt(1, n0, 2)
+        def tiles(h, *ns):
+            return [(h, n) for n in ns]
+        def place(ts, banks):
+            for tile, bank in zip(ts, banks):
+                bank_of[tile] = bank
+        early = tiles(0, 4, 5, 6, 0, 1)
+        place(early, (4, 3, 2, 0, 1))
+        parked.update({(0, 4): None, (0, 5): None, (0, 6): None})
+        lent = (5, 6, 7)
+        tier_one(0, 0, 0, 256, x_raw[0, 0, 0, 256], 0, ((S, 0, 256),))
+        tier_one(0, 0, 256, 256, x_raw[0, 0, 256, 256], 0, ((S, 0, 256),))
+        tier_two(0, 0, (6, 7, 5, 1))
+        tier_one(0, 1, 0, 256, x_raw[0, 1, 0, 512], 0, ((S, 0, 256),))
+        tier_one(0, 1, 256, 256, x_raw[0, 1, 0, 512], 256, ((S, 0, 256),))
+        tier_two(0, 1, (6, 7, 5))
+        for h, a in ((1, 0), (1, 1)):
+            for u in range(2):
+                tier_one(h, a, 256 * u, 256, x_raw[h, a, 0, 512], 256 * u, ((S, 0, 256),))
+            tier_two(h, a, (7, 5, 6) if a == 0 else (5, 6, 7))
+        x_passes(early, every_x)
+        place(tiles(0, 2, 3, 7), (4, 3, 2))
+        x_passes(tiles(0, 2, 3, 7), every_x)
+        place(tiles(1, 0, 1, 2), (6, 7, 5))
+        x_passes(tiles(1, 0, 1, 2), every_x)
         gather_words(0)
+        quantize_wt(0, 0, 0, 2, ((S, 0, 256),))
+        quantize_wt(1, 0, 0, 2, ((S, 0, 256),))
         gather_words(1)
-
-        quantize_wt(0, (on_scalar, on_scalar))
-        quantize_wt(1, (on_scalar, on_scalar))
-        tab_passes(0, pairs[0])
-        tab_passes(0, pairs[1])
-        quantize_wt(2, (on_vector, on_vector), one_stage=True)
-        tab_passes(1, pairs[0])
-        tab_passes(0, pairs[2])
-        tier_one(1, 0, (on_vector, on_vector), one_stage=True)
-        quantize_wt(3, (on_scalar, on_scalar))
-        tier_one(1, 1, (on_scalar, on_vector))
-        tier_two(1, 0, pairs[1])
-        tab_passes(0, pairs[3])
-        tab_passes(1, pairs[2])
-        x_passes(1, pairs[0] + pairs[2], every_x[:1])
-        tier_two(1, 1, pairs[1])
-        tab_passes(1, pairs[3])
-        x_passes(1, pairs[3], every_x[:1])
-        x_passes(1, pairs[0] + pairs[2] + pairs[3], every_x[1:])
-        for n in pairs[1]:
-            tab_passes(1, (n,))
-            x_passes(1, (n,), every_x)
+        tab_passes(tiles(0, 0, 1))
+        quantize_wt(0, 2, 0, 2, ((S, 0, 256),))
+        quantize_wt(1, 2, 0, 2, ((S, 0, 256),))
+        tab_passes(tiles(1, 0, 1))
+        for n0 in (4, 6):
+            quantize_wt(0, n0, 0, 2, ((V, 0, 256),))
+            quantize_wt(1, n0, 0, 2, ((V, 0, 256),))
+        place(tiles(1, 3, 4), (0, 1))
+        x_passes(tiles(1, 3, 4), every_x)
+        tab_passes(tiles(0, 2, 3))
+        tab_passes(tiles(1, 2, 3))
+        place(tiles(0, 4, 5), (6, 7))
+        tab_passes(tiles(0, 4, 5))
+        tab_passes(tiles(1, 4))
+        place(tiles(1, 5, 6, 7) + tiles(0, 6), (4, 3, 0, 5))
+        x_passes(tiles(1, 5), every_x)
+        tab_passes(tiles(1, 5))
+        tab_passes(tiles(0, 6, 7))
+        for n in (6, 7):
+            x_passes(tiles(1, n), every_x)
+            tab_passes(tiles(1, n))

@@ -31,11 +31,11 @@ ALIGN = 256
 
 
 def interleaved(ap):
-    return ap.rearrange("p (c i) t -> p c t i", i=4)
+    return ap.rearrange("p (c i) t -> p c t i", i=2)
 
 
 def planar(ap):
-    return ap.rearrange("p t (c i) -> p c t i", i=4)
+    return ap.rearrange("p t (c i) -> p c t i", i=2)
 
 
 def tile_list_tiert_gelu_kernel(
@@ -132,12 +132,12 @@ def tile_list_tiert_gelu_kernel(
             round_cols(raw[:, :, off : off + width], grouped, shares)
             quantize(grouped[:], words[:, col0 : col0 + width], scales[:, col0 : col0 + width])
 
-        def tier_two(h, a, banks, reuse=None):
+        def tier_two(h, a, banks):
             q_words, q_scales = xq[h, a]
             words = keep([P, HALF], U32, f"xr_w{h}{a}")
             scales = keep([P, HALF], U8, f"xr_sc{h}{a}")
             xr[h, a] = (words, scales)
-            left = keep([P, HALF, PACK], BF16, f"left{h}{a}", reuse)
+            left = keep([P, HALF, PACK], BF16, f"left{h}{a}", f"xq_bf{h}{a}2")
             for s in range(HALF // P):
                 cols = slice(s * P, (s + 1) * P)
                 back = psum.tile([P, PACK, P], F32, name="back", tag=f"bank{banks[s % len(banks)]}")
@@ -243,40 +243,40 @@ def tile_list_tiert_gelu_kernel(
         gather_scales()
         for a in range(PASSES):
             nc.vector.memset(tab_sc[a][:].bitcast(I32), 0)
-        with nc.allow_non_contiguous_dma(reason="one bias value a partition and tile"):
-            nc.sync.dma_start(bias[:], b.rearrange("(c p) -> p c", p=P))
+        move_scales(0, nc.sync)
         load_table()
         load_wt(0, 0, 2)
-        move_scales(0, nc.gpsimd)
         load_wt(1, 0, 2)
-        move_scales(1, nc.gpsimd)
-        for n0 in (2, 4, 6):
-            load_wt(0, n0, 2)
-            load_wt(1, n0, 2)
+        move_scales(1, nc.sync)
+        load_wt(0, 2, 2)
+        load_wt(1, 2, 2)
+        with nc.allow_non_contiguous_dma(reason="one bias value a partition and tile"):
+            nc.sync.dma_start(bias[:], b.rearrange("(c p) -> p c", p=P))
+        load_wt(0, 4, 2)
+        load_wt(1, 4, 2)
+        load_wt(0, 6, 2)
+        load_wt(1, 6, 2)
         def tiles(h, *ns):
             return [(h, n) for n in ns]
         def place(ts, banks):
             for tile, bank in zip(ts, banks):
                 bank_of[tile] = bank
-        early = tiles(0, 4, 5, 6, 0, 1)
-        place(early, (4, 3, 2, 0, 1))
-        parked.update({(0, 4): None, (0, 5): None, (0, 6): None})
-        lent = (5, 6, 7)
-        tier_one(0, 0, 0, 256, x_raw[0, 0, 0, 256], 0, ((S, 0, 256),))
-        tier_one(0, 0, 256, 256, x_raw[0, 0, 256, 256], 0, ((S, 0, 256),))
-        tier_two(0, 0, (6, 7, 5, 1))
-        tier_one(0, 1, 0, 256, x_raw[0, 1, 0, 512], 0, ((S, 0, 256),))
-        tier_one(0, 1, 256, 256, x_raw[0, 1, 0, 512], 256, ((S, 0, 256),))
-        tier_two(0, 1, (6, 7, 5))
-        for h, a in ((1, 0), (1, 1)):
+        early = tiles(0, 4, 5, 6, 7, 0, 1)
+        place(early, (2, 3, 4, 5, 0, 1))
+        parked.update({tile: None for tile in early[:4]})
+        for u in range(2):
+            tier_one(0, 0, 256 * u, 256, x_raw[0, 0, 256 * u, 256], 0, ((S, 0, 256),))
+        tier_two(0, 0, (6, 7, 0, 1))
+        for h, a in ((0, 1), (1, 0), (1, 1)):
             for u in range(2):
                 tier_one(h, a, 256 * u, 256, x_raw[h, a, 0, 512], 256 * u, ((S, 0, 256),))
-            tier_two(h, a, (7, 5, 6) if a == 0 else (5, 6, 7))
-        x_passes(early, every_x)
-        place(tiles(0, 2, 3, 7), (4, 3, 2))
-        x_passes(tiles(0, 2, 3, 7), every_x)
-        place(tiles(1, 0, 1, 2), (6, 7, 5))
-        x_passes(tiles(1, 0, 1, 2), every_x)
+            if (h, a) == (1, 1):
+                x_passes(early, every_x)
+            tier_two(h, a, {(0, 1): (0, 1, 6, 7), (1, 0): (6, 7), (1, 1): (4, 5, 6, 7)}[h, a])
+        place(tiles(0, 2, 3), (2, 3))
+        x_passes(tiles(0, 2, 3), every_x)
+        place(tiles(1, 0, 1, 2, 3), (4, 5, 6, 7))
+        x_passes(tiles(1, 0, 1, 2, 3), every_x)
         gather_words(0)
         quantize_wt(0, 0, 0, 2, ((S, 0, 256),))
         quantize_wt(1, 0, 0, 2, ((S, 0, 256),))
@@ -288,16 +288,13 @@ def tile_list_tiert_gelu_kernel(
         for n0 in (4, 6):
             quantize_wt(0, n0, 0, 2, ((V, 0, 256),))
             quantize_wt(1, n0, 0, 2, ((V, 0, 256),))
-        place(tiles(1, 3, 4), (0, 1))
-        x_passes(tiles(1, 3, 4), every_x)
         tab_passes(tiles(0, 2, 3))
         tab_passes(tiles(1, 2, 3))
-        place(tiles(0, 4, 5), (6, 7))
+        place(tiles(1, 4, 5) + tiles(0, 4, 5), (0, 1, 4, 5))
+        x_passes(tiles(1, 4, 5), every_x)
         tab_passes(tiles(0, 4, 5))
-        tab_passes(tiles(1, 4))
-        place(tiles(1, 5, 6, 7) + tiles(0, 6), (4, 3, 0, 5))
-        x_passes(tiles(1, 5), every_x)
-        tab_passes(tiles(1, 5))
+        tab_passes(tiles(1, 4, 5))
+        place(tiles(0, 6, 7) + tiles(1, 6, 7), (2, 3, 6, 7))
         tab_passes(tiles(0, 6, 7))
         for n in (6, 7):
             x_passes(tiles(1, n), every_x)

@@ -31,11 +31,11 @@ ALIGN = 256
 
 
 def interleaved(ap):
-    return ap.rearrange("p (c i) t -> p c t i", i=2)
+    return ap.rearrange("p (c i) t -> p c t i", i=4)
 
 
 def planar(ap):
-    return ap.rearrange("p t (c i) -> p c t i", i=2)
+    return ap.rearrange("p t (c i) -> p c t i", i=4)
 
 
 def tile_list_tiert_gelu_kernel(
@@ -132,7 +132,7 @@ def tile_list_tiert_gelu_kernel(
             round_cols(raw[:, :, off : off + width], grouped, shares)
             quantize(grouped[:], words[:, col0 : col0 + width], scales[:, col0 : col0 + width])
 
-        def tier_two(h, a, banks):
+        def subtract(h, a, banks):
             q_words, q_scales = xq[h, a]
             words = keep([P, HALF], U32, f"xr_w{h}{a}")
             scales = keep([P, HALF], U8, f"xr_sc{h}{a}")
@@ -152,26 +152,67 @@ def tile_list_tiert_gelu_kernel(
                         stop=True,
                     )
                 nc.vector.tensor_tensor(interleaved(left[:, cols, :]), planar(x_raw[h, a, s]), planar(back[:]), SUB)
-            quantize(left[:], words[:], scales[:])
+            return lambda: quantize(left[:], words[:], scales[:])
 
-        def quantize_wt(a, n0, off, tiles, shares, reuse=None):
+        def subtract_by_quarters(h, a, banks):
+            q_words, q_scales = xq[h, a]
+            words = keep([P, HALF], U32, f"xr_w{h}{a}")
+            scales = keep([P, HALF], U8, f"xr_sc{h}{a}")
+            xr[h, a] = (words, scales)
+            left = keep([P, HALF, PACK], BF16, f"left{h}{a}", f"xq_bf{h}{a}2")
+            for s in range(HALF // P + 1):
+                if s < HALF // P:
+                    cols = slice(s * P, (s + 1) * P)
+                    back = psum.tile([P, PACK, P], F32, name="back", tag=f"bank{banks[s % len(banks)]}")
+                    for t in range(PACK):
+                        nc.tensor.matmul_mx(
+                            back[:, t, :],
+                            lhsT=eye_w[:, t * P : (t + 1) * P].bitcast(FP8X4),
+                            lhsT_scale=eye_sc[:, t * P : (t + 1) * P],
+                            rhs=q_words[:, cols].bitcast(FP8X4),
+                            rhs_scale=q_scales[:, cols],
+                            start=True,
+                            stop=True,
+                        )
+                    nc.vector.tensor_tensor(
+                        interleaved(left[:, cols, :]), planar(x_raw[h, a, s]), planar(back[:]), SUB
+                    )
+                if s > 0:
+                    cols = slice((s - 1) * P, s * P)
+                    quantize(left[:, cols, :], words[:, cols], scales[:, cols])
+
+        def quarter_passes(tiles, tier, a):
+            for s in range(HALF // P):
+                cols = slice(s * P, (s + 1) * P)
+                for h, n in tiles:
+                    words, scales = tier[h, a]
+                    nc.tensor.matmul_mx(
+                        acc[h, n][:, cols],
+                        lhsT=wx_w[a][:, 2 * n * P : 2 * (n + 1) * P].bitcast(FP4X4),
+                        lhsT_scale=wx_sc[:, a, n * P : (n + 1) * P],
+                        rhs=words[:, cols].bitcast(FP8X4), rhs_scale=scales[:, cols], start=False, stop=False,
+                    )
+            for tile in tiles:
+                done[tile] = done[tile] + 1
+
+        def round_wt(a, n0, off, tiles, shares, reuse=None):
             name = f"wq{a}{n0 + off}"
             words, scales = keep([P, tiles * P], U32, name + "_w"), keep([P, tiles * P], U8, name + "_sc")
             grouped = keep([P, tiles * P, PACK], BF16, name + "_bf", reuse)
             round_cols(wt_raw[a, n0][:, :, off * P : (off + tiles) * P], grouped, shares)
-            quantize(grouped[:], words[:], scales[:])
             for i in range(tiles):
                 wq[n0 + off + i, a] = (words[:, i * P : (i + 1) * P], scales[:, i * P : (i + 1) * P])
+            return lambda: quantize(grouped[:], words[:], scales[:])
 
         def gather_scales():
             nc.vector.tensor_copy(picked_sc[:], scale_window[:].indirect(offsets[:]))
 
         def gather_words(h):
-            picked = keep([P, HALF], U32, f"picked_w{h}", "picked_w0")
+            picked = keep([P, HALF], U32, f"picked_w{h}", "picked_w")
             entries = offsets[:, h * HALF // LIST_ROWS : (h + 1) * HALF // LIST_ROWS]
             nc.vector.tensor_copy(picked[:], word_window[:].indirect(entries))
             tab_w[h] = keep([P, PASSES, 2 * HALF], U8, f"tab_w{h}")
-            nc.vector.tensor_copy(
+            return lambda: nc.vector.tensor_copy(
                 tab_w[h][:].bitcast(U16), picked[:].bitcast(U16).rearrange("p (j a) -> p a j", a=PASSES)
             )
 
@@ -197,8 +238,11 @@ def tile_list_tiert_gelu_kernel(
                     total = parked[h, n]
                     nc.vector.tensor_tensor(total[:], total[:], acc[h, n][:], ADD)
                 result = keep([P, HALF], F32, f"result{h}{n}", spare.pop() if spare else None)
-                nc.scalar.activation(result[:], total[:], GELU, bias=bias[:, n : n + 1])
-                nc.sync.dma_start(out[n * P : (n + 1) * P, h * HALF : (h + 1) * HALF], result[:])
+                parts = 2 if (h, n) == (1, N // P - 1) else 1
+                for part in range(parts):
+                    cols = slice(part * HALF // parts, (part + 1) * HALF // parts)
+                    nc.scalar.activation(result[:, cols], total[:, cols], GELU, bias=bias[:, n : n + 1])
+                    nc.sync.dma_start(out[n * P : (n + 1) * P, h * HALF : (h + 1) * HALF][:, cols], result[:, cols])
 
         parked = {}
         spare = [f"xq_bf{h}{a}{s}" for h in (1, 0) for a in (1, 0) for s in (2, 0)]
@@ -243,17 +287,17 @@ def tile_list_tiert_gelu_kernel(
         gather_scales()
         for a in range(PASSES):
             nc.vector.memset(tab_sc[a][:].bitcast(I32), 0)
-        move_scales(0, nc.sync)
-        load_table()
         load_wt(0, 0, 2)
         load_wt(1, 0, 2)
-        move_scales(1, nc.sync)
+        load_table()
+        move_scales(0, nc.sync)
         load_wt(0, 2, 2)
+        move_scales(1, nc.sync)
         load_wt(1, 2, 2)
-        with nc.allow_non_contiguous_dma(reason="one bias value a partition and tile"):
-            nc.sync.dma_start(bias[:], b.rearrange("(c p) -> p c", p=P))
         load_wt(0, 4, 2)
         load_wt(1, 4, 2)
+        with nc.allow_non_contiguous_dma(reason="one bias value a partition and tile"):
+            nc.sync.dma_start(bias[:], b.rearrange("(c p) -> p c", p=P))
         load_wt(0, 6, 2)
         load_wt(1, 6, 2)
         def tiles(h, *ns):
@@ -261,41 +305,65 @@ def tile_list_tiert_gelu_kernel(
         def place(ts, banks):
             for tile, bank in zip(ts, banks):
                 bank_of[tile] = bank
-        early = tiles(0, 4, 5, 6, 7, 0, 1)
+        early = tiles(0, 4, 5, 6, 7, 2, 3)
         place(early, (2, 3, 4, 5, 0, 1))
-        parked.update({tile: None for tile in early[:4]})
-        for u in range(2):
-            tier_one(0, 0, 256 * u, 256, x_raw[0, 0, 256 * u, 256], 0, ((S, 0, 256),))
-        tier_two(0, 0, (6, 7, 0, 1))
-        for h, a in ((0, 1), (1, 0), (1, 1)):
-            for u in range(2):
+        parked.update({tile: None for tile in early})
+        def x_half(h, a, u):
+            if (h, a) == (0, 0):
+                tier_one(0, 0, 256 * u, 256, x_raw[0, 0, 256 * u, 256], 0, ((S, 0, 256),))
+            else:
                 tier_one(h, a, 256 * u, 256, x_raw[h, a, 0, 512], 256 * u, ((S, 0, 256),))
-            if (h, a) == (1, 1):
-                x_passes(early, every_x)
-            tier_two(h, a, {(0, 1): (0, 1, 6, 7), (1, 0): (6, 7), (1, 1): (4, 5, 6, 7)}[h, a])
-        place(tiles(0, 2, 3), (2, 3))
-        x_passes(tiles(0, 2, 3), every_x)
-        place(tiles(1, 0, 1, 2, 3), (4, 5, 6, 7))
-        x_passes(tiles(1, 0, 1, 2, 3), every_x)
-        gather_words(0)
-        quantize_wt(0, 0, 0, 2, ((S, 0, 256),))
-        quantize_wt(1, 0, 0, 2, ((S, 0, 256),))
-        gather_words(1)
-        tab_passes(tiles(0, 0, 1))
-        quantize_wt(0, 2, 0, 2, ((S, 0, 256),))
-        quantize_wt(1, 2, 0, 2, ((S, 0, 256),))
+        x_half(0, 0, 0)
+        x_half(0, 0, 1)
+        subtract_by_quarters(0, 0, (6, 7, 1))
+        x_half(0, 1, 0)
+        x_half(0, 1, 1)
+        finish = subtract(0, 1, (7, 1, 6))
+        x_half(1, 0, 0)
+        finish()
+        x_half(1, 0, 1)
+        finish = subtract(1, 0, (6, 7))
+        x_half(1, 1, 0)
+        finish()
+        x_half(1, 1, 1)
+        x_passes(early[:5], every_x[:1])
+        quarter_passes(early[:4], xr, 0)
+        x_passes(early[:5], every_x[2:3])
+        x_passes(early[4:5], every_x[1:2])
+        x_passes(early[5:], every_x[:3])
+        x_passes(early, every_x[3:])
+        finish = subtract(1, 1, (4, 5, 6, 7))
+        first_pair = [round_wt(a, 0, 0, 2, ((S, 0, 256),)) for a in range(2)]
+        first_pair[0]()
+        finish()
+        part = gather_words(1)
+        first_pair[1]()
+        part()
+        place(tiles(0, 0, 1), (2, 3))
+        x_passes(tiles(0, 0, 1), every_x)
+        place(tiles(1, 0, 1, 2, 3, 4, 5), (0, 1, 4, 5, 6, 7))
+        x_passes(tiles(1, 0, 1, 2, 3, 4, 5), every_x)
+        second_pair = [round_wt(a, 2, 0, 2, ((S, 0, 256),)) for a in range(2)]
+        second_pair[0]()
+        part = gather_words(0)
+        second_pair[1]()
+        part()
+        third_pair = [round_wt(a, 4, 0, 2, ((S, 0, 256),)) for a in range(2)]
+        for finish in third_pair:
+            finish()
         tab_passes(tiles(1, 0, 1))
-        for n0 in (4, 6):
-            quantize_wt(0, n0, 0, 2, ((V, 0, 256),))
-            quantize_wt(1, n0, 0, 2, ((V, 0, 256),))
-        tab_passes(tiles(0, 2, 3))
         tab_passes(tiles(1, 2, 3))
-        place(tiles(1, 4, 5) + tiles(0, 4, 5), (0, 1, 4, 5))
-        x_passes(tiles(1, 4, 5), every_x)
-        tab_passes(tiles(0, 4, 5))
+        last_pair = [round_wt(a, 6, 0, 2, ((V, 0, 256),)) for a in range(2)]
+        for finish in last_pair:
+            finish()
+        tab_passes(tiles(0, 0, 1))
+        place(tiles(0, 2, 3), (0, 1))
+        tab_passes(tiles(0, 2, 3))
         tab_passes(tiles(1, 4, 5))
-        place(tiles(0, 6, 7) + tiles(1, 6, 7), (2, 3, 6, 7))
+        place(tiles(0, 4, 5) + tiles(1, 6, 7) + tiles(0, 6, 7), (4, 5, 2, 3, 0, 1))
+        tab_passes(tiles(0, 4, 5))
+        x_passes(tiles(1, 6), every_x)
         tab_passes(tiles(0, 6, 7))
-        for n in (6, 7):
-            x_passes(tiles(1, n), every_x)
-            tab_passes(tiles(1, n))
+        tab_passes(tiles(1, 6))
+        x_passes(tiles(1, 7), every_x)
+        tab_passes(tiles(1, 7))

@@ -67,6 +67,8 @@ def tile_list_tiert_gelu_kernel(
         picked_sc = keep([P, J], U8, "picked_sc")
         tab_sc = [keep([P, J], U8, f"tab_sc{a}") for a in range(PASSES)]
         bias = keep([P, N // P], F32, "bias")
+        b_rows = keep([P, P], F32, "b_rows")
+        identity = keep([P, P], F32, "identity")
         eye_w = keep([P, PACK * P], U32, "eye_w")
         eye_sc = keep([P, PACK * P], U8, "eye_sc")
         first_row = P - SCALE_ROWS
@@ -117,8 +119,14 @@ def tile_list_tiert_gelu_kernel(
                 out=low, in_=low, compare_op=mybir.AluOpType.not_equal, fill=1.0,
                 base=0, pattern=[[-1, 2], [1, K_PASS]], channel_multiplier=-PACK,
             )
+            nc.scalar.copy(identity[:], eye[:, LEAD : LEAD + K_PASS : PACK])
             nc.vector.tensor_copy(eye[:, LEAD + two :], eye[:, LEAD - 2 : LEAD - 2 + two])
             nc.vector.quantize_mx(eye_w[:].bitcast(FP8X4), eye_sc[:], eye[:, LEAD:])
+
+        def make_bias(bank):
+            b_bank = psum.tile([P, PACK, P], F32, name="b_bank", tag=f"bank{bank}")
+            nc.tensor.transpose(b_bank[:, 0, :], b_rows[:], identity[:])
+            nc.scalar.copy(bias[:], b_bank[:, 0, 0 : N // P])
 
         def round_cols(raw, grouped, shares):
             for copy, c0, c1 in shares:
@@ -271,11 +279,13 @@ def tile_list_tiert_gelu_kernel(
         every_x = ((xq, 0), (xr, 0), (xq, 1), (xr, 1))
         S, V = on_scalar, on_vector
 
+        nc.vector.memset(b_rows[:], 0.0)
         nc.vector.memset(wx_sc[:].bitcast(I32), 0)
         nc.vector.memset(scale_window[0:first_row, :].bitcast(I32), 0)
         make_eye()
         nc.sync.dma_start(offsets[:], offs)
         load_tab_scales()
+        nc.sync.dma_start(b_rows[0 : N // P, :], b.rearrange("(c p) -> c p", p=P))
         load_x(0, 0, 0, 256)
         load_x(0, 0, 256, 256)
         load_wx(0)
@@ -290,14 +300,12 @@ def tile_list_tiert_gelu_kernel(
         load_wt(0, 0, 2)
         load_wt(1, 0, 2)
         load_table()
-        move_scales(0, nc.sync)
         load_wt(0, 2, 2)
-        move_scales(1, nc.sync)
         load_wt(1, 2, 2)
         load_wt(0, 4, 2)
+        move_scales(1, nc.sync)
         load_wt(1, 4, 2)
-        with nc.allow_non_contiguous_dma(reason="one bias value a partition and tile"):
-            nc.sync.dma_start(bias[:], b.rearrange("(c p) -> p c", p=P))
+        move_scales(0, nc.sync)
         load_wt(0, 6, 2)
         load_wt(1, 6, 2)
         def tiles(h, *ns):
@@ -305,6 +313,7 @@ def tile_list_tiert_gelu_kernel(
         def place(ts, banks):
             for tile, bank in zip(ts, banks):
                 bank_of[tile] = bank
+        make_bias(5)
         early = tiles(0, 4, 5, 6, 7, 2, 3)
         place(early, (2, 3, 4, 5, 0, 1))
         parked.update({tile: None for tile in early})
@@ -315,10 +324,10 @@ def tile_list_tiert_gelu_kernel(
                 tier_one(h, a, 256 * u, 256, x_raw[h, a, 0, 512], 256 * u, ((S, 0, 256),))
         x_half(0, 0, 0)
         x_half(0, 0, 1)
-        subtract_by_quarters(0, 0, (6, 7, 1))
+        subtract_by_quarters(0, 0, (0, 1, 6, 7))
         x_half(0, 1, 0)
         x_half(0, 1, 1)
-        finish = subtract(0, 1, (7, 1, 6))
+        finish = subtract(0, 1, (1, 6, 7))
         x_half(1, 0, 0)
         finish()
         x_half(1, 0, 1)
@@ -360,10 +369,9 @@ def tile_list_tiert_gelu_kernel(
         place(tiles(0, 2, 3), (0, 1))
         tab_passes(tiles(0, 2, 3))
         tab_passes(tiles(1, 4, 5))
-        place(tiles(0, 4, 5) + tiles(1, 6, 7) + tiles(0, 6, 7), (4, 5, 2, 3, 0, 1))
+        place(tiles(0, 4, 5, 6, 7) + tiles(1, 6, 7), (4, 5, 2, 3, 0, 1))
         tab_passes(tiles(0, 4, 5))
-        x_passes(tiles(1, 6), every_x)
         tab_passes(tiles(0, 6, 7))
-        tab_passes(tiles(1, 6))
-        x_passes(tiles(1, 7), every_x)
-        tab_passes(tiles(1, 7))
+        for n in (6, 7):
+            x_passes(tiles(1, n), every_x)
+            tab_passes(tiles(1, n))

@@ -64,7 +64,6 @@ def tile_list_tiert_gelu_kernel(
         wx_sc = keep([P, PASSES, N], U8, "wx_sc")
         scale_window = keep([P, T], U8, "scale_window")
         word_window = keep([P, T], U32, "word_window")
-        picked_sc = keep([P, J], U8, "picked_sc")
         tab_sc = [keep([P, J], U8, f"tab_sc{a}") for a in range(PASSES)]
         bias = keep([P, N // P], F32, "bias")
         b_rows = keep([P, P], F32, "b_rows")
@@ -80,7 +79,8 @@ def tile_list_tiert_gelu_kernel(
             raw = load_rows(x, a, h * HALF + col0, width, f"x_raw{h}{a}{col0 // P}")
             for s in range(width // P):
                 x_raw[h, a, col0 // P + s] = raw[:, :, s * P : (s + 1) * P]
-            x_raw[h, a, col0, width] = raw
+            for u in range(width // UNIT):
+                x_raw[h, a, "unit", col0 // UNIT + u] = raw[:, :, u * UNIT : (u + 1) * UNIT]
 
         def load_wt(a, n0, tiles):
             wt_raw[a, n0] = load_rows(wt, a, n0 * P, tiles * P, f"wt_raw{a}{n0}")
@@ -103,7 +103,7 @@ def tile_list_tiert_gelu_kernel(
         def load_table():
             nc.sync.dma_start(word_window[:].bitcast(I32), tab_words[0].rearrange("p t c -> p (t c)").bitcast(I32))
 
-        def move_scales(a, queue):
+        def move_scales(picked_sc, a, queue):
             for r in range(4):
                 row = first_row + 16 * a + r
                 queue.dma_start(
@@ -132,62 +132,40 @@ def tile_list_tiert_gelu_kernel(
             for copy, c0, c1 in shares:
                 copy(interleaved(grouped[:, c0:c1, :]), planar(raw[:, :, c0:c1]))
 
-        def tier_one(h, a, col0, width, raw, off, shares, reuse=None):
+        left = {}
+
+        def round_x(h, a, u, shares):
             if (h, a) not in xq:
                 xq[h, a] = (keep([P, HALF], U32, f"xq_w{h}{a}"), keep([P, HALF], U8, f"xq_sc{h}{a}"))
+                xr[h, a] = (keep([P, HALF], U32, f"xr_w{h}{a}"), keep([P, HALF], U8, f"xr_sc{h}{a}"))
             words, scales = xq[h, a]
-            grouped = keep([P, width, PACK], BF16, f"xq_bf{h}{a}{col0 // P}", reuse)
-            round_cols(raw[:, :, off : off + width], grouped, shares)
-            quantize(grouped[:], words[:, col0 : col0 + width], scales[:, col0 : col0 + width])
+            grouped = keep([P, UNIT, PACK], BF16, f"xq_bf{h}{a}{2 * u}")
+            round_cols(x_raw[h, a, "unit", u], grouped, shares)
+            cols = slice(u * UNIT, (u + 1) * UNIT)
+            return lambda: quantize(grouped[:], words[:, cols], scales[:, cols])
 
-        def subtract(h, a, banks):
-            q_words, q_scales = xq[h, a]
-            words = keep([P, HALF], U32, f"xr_w{h}{a}")
-            scales = keep([P, HALF], U8, f"xr_sc{h}{a}")
-            xr[h, a] = (words, scales)
-            left = keep([P, HALF, PACK], BF16, f"left{h}{a}", f"xq_bf{h}{a}2")
-            for s in range(HALF // P):
-                cols = slice(s * P, (s + 1) * P)
-                back = psum.tile([P, PACK, P], F32, name="back", tag=f"bank{banks[s % len(banks)]}")
-                for t in range(PACK):
-                    nc.tensor.matmul_mx(
-                        back[:, t, :],
-                        lhsT=eye_w[:, t * P : (t + 1) * P].bitcast(FP8X4),
-                        lhsT_scale=eye_sc[:, t * P : (t + 1) * P],
-                        rhs=q_words[:, cols].bitcast(FP8X4),
-                        rhs_scale=q_scales[:, cols],
-                        start=True,
-                        stop=True,
-                    )
-                nc.vector.tensor_tensor(interleaved(left[:, cols, :]), planar(x_raw[h, a, s]), planar(back[:]), SUB)
-            return lambda: quantize(left[:], words[:], scales[:])
+        def take_back(h, a, s, bank):
+            words, scales = xq[h, a]
+            if s == 0:
+                left[h, a] = keep([P, HALF, PACK], BF16, f"left{h}{a}", f"xq_bf{h}{a}2")
+            cols = slice(s * P, (s + 1) * P)
+            back = psum.tile([P, PACK, P], F32, name="back", tag=f"bank{bank}")
+            for t in range(PACK):
+                nc.tensor.matmul_mx(
+                    back[:, t, :],
+                    lhsT=eye_w[:, t * P : (t + 1) * P].bitcast(FP8X4),
+                    lhsT_scale=eye_sc[:, t * P : (t + 1) * P],
+                    rhs=words[:, cols].bitcast(FP8X4),
+                    rhs_scale=scales[:, cols],
+                    start=True,
+                    stop=True,
+                )
+            nc.vector.tensor_tensor(interleaved(left[h, a][:, cols, :]), planar(x_raw[h, a, s]), planar(back[:]), SUB)
 
-        def subtract_by_quarters(h, a, banks):
-            q_words, q_scales = xq[h, a]
-            words = keep([P, HALF], U32, f"xr_w{h}{a}")
-            scales = keep([P, HALF], U8, f"xr_sc{h}{a}")
-            xr[h, a] = (words, scales)
-            left = keep([P, HALF, PACK], BF16, f"left{h}{a}", f"xq_bf{h}{a}2")
-            for s in range(HALF // P + 1):
-                if s < HALF // P:
-                    cols = slice(s * P, (s + 1) * P)
-                    back = psum.tile([P, PACK, P], F32, name="back", tag=f"bank{banks[s % len(banks)]}")
-                    for t in range(PACK):
-                        nc.tensor.matmul_mx(
-                            back[:, t, :],
-                            lhsT=eye_w[:, t * P : (t + 1) * P].bitcast(FP8X4),
-                            lhsT_scale=eye_sc[:, t * P : (t + 1) * P],
-                            rhs=q_words[:, cols].bitcast(FP8X4),
-                            rhs_scale=q_scales[:, cols],
-                            start=True,
-                            stop=True,
-                        )
-                    nc.vector.tensor_tensor(
-                        interleaved(left[:, cols, :]), planar(x_raw[h, a, s]), planar(back[:]), SUB
-                    )
-                if s > 0:
-                    cols = slice((s - 1) * P, s * P)
-                    quantize(left[:, cols, :], words[:, cols], scales[:, cols])
+        def quantize_left(h, a, first=0, end=HALF // P):
+            words, scales = xr[h, a]
+            cols = slice(first * P, end * P)
+            quantize(left[h, a][:, cols, :], words[:, cols], scales[:, cols])
 
         def quarter_passes(tiles, tier, a):
             for s in range(HALF // P):
@@ -212,8 +190,10 @@ def tile_list_tiert_gelu_kernel(
                 wq[n0 + off + i, a] = (words[:, i * P : (i + 1) * P], scales[:, i * P : (i + 1) * P])
             return lambda: quantize(grouped[:], words[:], scales[:])
 
-        def gather_scales():
+        def gather_scales(reuse):
+            picked_sc = keep([P, J], U8, "picked_sc", reuse)
             nc.vector.tensor_copy(picked_sc[:], scale_window[:].indirect(offsets[:]))
+            return picked_sc
 
         def gather_words(h):
             picked = keep([P, HALF], U32, f"picked_w{h}", "picked_w")
@@ -283,68 +263,79 @@ def tile_list_tiert_gelu_kernel(
         nc.vector.memset(wx_sc[:].bitcast(I32), 0)
         nc.vector.memset(scale_window[0:first_row, :].bitcast(I32), 0)
         make_eye()
-        nc.sync.dma_start(offsets[:], offs)
-        load_tab_scales()
         nc.sync.dma_start(b_rows[0 : N // P, :], b.rearrange("(c p) -> c p", p=P))
         load_x(0, 0, 0, 256)
         load_x(0, 0, 256, 256)
         load_wx(0)
         load_wx_scales(nc.sync)
-        load_x(0, 1, 0, 512)
+        load_x(0, 1, 0, 256)
+        load_x(0, 1, 256, 256)
         load_wx(1)
         load_x(1, 0, 0, 512)
         load_x(1, 1, 0, 512)
-        gather_scales()
+        nc.sync.dma_start(offsets[:], offs)
+        load_tab_scales()
         for a in range(PASSES):
             nc.vector.memset(tab_sc[a][:].bitcast(I32), 0)
         load_wt(0, 0, 2)
         load_wt(1, 0, 2)
         load_table()
-        load_wt(0, 2, 2)
-        load_wt(1, 2, 2)
-        load_wt(0, 4, 2)
-        move_scales(1, nc.sync)
-        load_wt(1, 4, 2)
-        move_scales(0, nc.sync)
-        load_wt(0, 6, 2)
-        load_wt(1, 6, 2)
+        for n0 in (2, 4):
+            load_wt(0, n0, 2)
+            load_wt(1, n0, 2)
+
         def tiles(h, *ns):
             return [(h, n) for n in ns]
         def place(ts, banks):
             for tile, bank in zip(ts, banks):
                 bank_of[tile] = bank
+        whole = lambda copy: ((copy, 0, UNIT),)
         make_bias(5)
         early = tiles(0, 4, 5, 6, 7, 2, 3)
         place(early, (2, 3, 4, 5, 0, 1))
         parked.update({tile: None for tile in early})
-        def x_half(h, a, u):
-            if (h, a) == (0, 0):
-                tier_one(0, 0, 256 * u, 256, x_raw[0, 0, 256 * u, 256], 0, ((S, 0, 256),))
-            else:
-                tier_one(h, a, 256 * u, 256, x_raw[h, a, 0, 512], 256 * u, ((S, 0, 256),))
-        x_half(0, 0, 0)
-        x_half(0, 0, 1)
-        subtract_by_quarters(0, 0, (0, 1, 6, 7))
-        x_half(0, 1, 0)
-        x_half(0, 1, 1)
-        finish = subtract(0, 1, (1, 6, 7))
-        x_half(1, 0, 0)
-        finish()
-        x_half(1, 0, 1)
-        finish = subtract(1, 0, (6, 7))
-        x_half(1, 1, 0)
-        finish()
-        x_half(1, 1, 1)
+        for u in range(2):
+            round_x(0, 0, u, ((S, 0, 96), (V, 96, UNIT)))()
+        for s, bank in enumerate((0, 1, 6, 7)):
+            take_back(0, 0, s, bank)
+            if s > 0:
+                quantize_left(0, 0, s - 1, s)
+        quantize_left(0, 0, 3, 4)
+        for u in range(2):
+            round_x(0, 1, u, whole(S))()
+        for s, bank in enumerate((1, 6, 7, 1)):
+            take_back(0, 1, s, bank)
+        third = [round_x(1, 0, u, whole(S)) for u in range(2)]
+        third[0]()
+        quantize_left(0, 1)
+        third[1]()
+        take_back(1, 0, 0, 6)
+        take_back(1, 0, 1, 7)
+        fourth = [round_x(1, 1, u, whole(S)) for u in range(2)]
+        take_back(1, 0, 2, 6)
+        take_back(1, 0, 3, 7)
         x_passes(early[:5], every_x[:1])
         quarter_passes(early[:4], xr, 0)
         x_passes(early[:5], every_x[2:3])
         x_passes(early[4:5], every_x[1:2])
         x_passes(early[5:], every_x[:3])
-        x_passes(early, every_x[3:])
-        finish = subtract(1, 1, (4, 5, 6, 7))
-        first_pair = [round_wt(a, 0, 0, 2, ((S, 0, 256),)) for a in range(2)]
+        x_passes(early[:2], every_x[3:])
+
+        x_passes(early[2:], every_x[3:])
+        fourth[0]()
+        quantize_left(1, 0)
+        fourth[1]()
+        for s, bank in enumerate((4, 5, 6, 7)):
+            take_back(1, 1, s, bank)
+        first_pair = [round_wt(a, 0, 0, 2, whole(S)) for a in range(2)]
+
+        picked_sc = gather_scales("x_raw110")
+        move_scales(picked_sc, 1, nc.sync)
+        move_scales(picked_sc, 0, nc.sync)
+        load_wt(0, 6, 2)
+        load_wt(1, 6, 2)
+        quantize_left(1, 1)
         first_pair[0]()
-        finish()
         part = gather_words(1)
         first_pair[1]()
         part()
@@ -352,17 +343,17 @@ def tile_list_tiert_gelu_kernel(
         x_passes(tiles(0, 0, 1), every_x)
         place(tiles(1, 0, 1, 2, 3, 4, 5), (0, 1, 4, 5, 6, 7))
         x_passes(tiles(1, 0, 1, 2, 3, 4, 5), every_x)
-        second_pair = [round_wt(a, 2, 0, 2, ((S, 0, 256),)) for a in range(2)]
+        second_pair = [round_wt(a, 2, 0, 2, whole(S)) for a in range(2)]
         second_pair[0]()
         part = gather_words(0)
         second_pair[1]()
         part()
-        third_pair = [round_wt(a, 4, 0, 2, ((S, 0, 256),)) for a in range(2)]
+        third_pair = [round_wt(a, 4, 0, 2, whole(S)) for a in range(2)]
         for finish in third_pair:
             finish()
         tab_passes(tiles(1, 0, 1))
         tab_passes(tiles(1, 2, 3))
-        last_pair = [round_wt(a, 6, 0, 2, ((V, 0, 256),)) for a in range(2)]
+        last_pair = [round_wt(a, 6, 0, 2, whole(V)) for a in range(2)]
         for finish in last_pair:
             finish()
         tab_passes(tiles(0, 0, 1))

@@ -16,17 +16,19 @@ FP4X4 = mybir.dt.float4_e2m1fn_x4
 GELU = mybir.ActivationFunctionType.Gelu_apprx_tanh
 SUB = mybir.AluOpType.subtract
 ADD = mybir.AluOpType.add
+MULT = mybir.AluOpType.mult
+EQUAL = mybir.AluOpType.is_equal
 
 P = 128
 PACK = 4
 K_PASS = P * PACK
 PASSES = 2
 QUADS = 4
+QUAD = 32
 HALF = 512
 UNIT = 256
 LIST_ROWS = 16
 SCALE_ROWS = PASSES * K_PASS // 32
-LEAD = 32
 ALIGN = 256
 
 
@@ -62,14 +64,10 @@ def tile_list_tiert_gelu_kernel(
         offsets = held.tile([P, J // LIST_ROWS], U16, name="offsets")
         wx_w = [keep([P, 2 * N], U8, f"wx_w{a}") for a in range(PASSES)]
         wx_sc = keep([P, PASSES, N], U8, "wx_sc")
-        scale_window = keep([P, T], U8, "scale_window")
         word_window = keep([P, T], U32, "word_window")
-        tab_sc = [keep([P, J], U8, f"tab_sc{a}") for a in range(PASSES)]
         bias = keep([P, N // P], F32, "bias")
-        b_rows = keep([P, P], F32, "b_rows")
-        identity = keep([P, P], F32, "identity")
         eye_w = keep([P, PACK * P], U32, "eye_w")
-        eye_sc = keep([P, PACK * P], U8, "eye_sc")
+        eye_sc = keep([P, 2 * P], U8, "eye_sc")
         first_row = P - SCALE_ROWS
         x_raw, wt_raw = {}, {}
         xq, xr, wq, tab_w = {}, {}, {}, {}
@@ -107,26 +105,33 @@ def tile_list_tiert_gelu_kernel(
             for r in range(4):
                 row = first_row + 16 * a + r
                 queue.dma_start(
-                    tab_sc[a][r:P:32, :].bitcast(I32), picked_sc[row : row + 13 : 4, :].bitcast(I32)
+                    tab_sc[r:P:32, a, :].bitcast(I32), picked_sc[row : row + 13 : 4, :].bitcast(I32)
                 )
 
         def make_eye():
-            eye = keep([P, LEAD + PACK * K_PASS], BF16, "eye")
-            two = 2 * K_PASS
-            nc.gpsimd.memset(eye[:, 0 : LEAD + two].bitcast(I32), 0)
-            low = eye[:, LEAD : LEAD + two].rearrange("p (t f) -> p t f", t=2)
-            nc.gpsimd.affine_select(
-                out=low, in_=low, compare_op=mybir.AluOpType.not_equal, fill=1.0,
-                base=0, pattern=[[-1, 2], [1, K_PASS]], channel_multiplier=-PACK,
-            )
-            nc.scalar.copy(identity[:], eye[:, LEAD : LEAD + K_PASS : PACK])
-            nc.vector.tensor_copy(eye[:, LEAD + two :], eye[:, LEAD - 2 : LEAD - 2 + two])
-            nc.vector.quantize_mx(eye_w[:].bitcast(FP8X4), eye_sc[:], eye[:, LEAD:])
-
-        def make_bias(bank):
-            b_bank = psum.tile([P, PACK, P], F32, name="b_bank", tag=f"bank{bank}")
-            nc.tensor.transpose(b_bank[:, 0, :], b_rows[:], identity[:])
-            nc.scalar.copy(bias[:], b_bank[:, 0, 0 : N // P])
+            two = 2 * QUAD
+            flags = keep([P, 2 * two], F32, "flags")
+            column = keep([P, two], F32, "column")
+            row = keep([P, QUAD], F32, "row")
+            eye = keep([P, 3 * K_PASS], BF16, "eye")
+            nc.vector.memset(flags[:, 0 : two + QUAD], 1.0)
+            nc.vector.memset(flags[:, two + QUAD : two + QUAD + 1], 0.0)
+            nc.vector.memset(flags[:, two + QUAD + 1 :], 1.0)
+            nc.vector.memset(eye[:, 0 : 2 * K_PASS].bitcast(I32), 0)
+            nc.vector.tensor_tensor_scan(column[:], flags[:, two:], flags[:, 0:two], 0.0, MULT, ADD)
+            nc.vector.memset(eye_w[:, 2 * P :], 0)
+            nc.vector.transpose(row[:], column[:, 0:QUAD])
+            nc.vector.memset(wx_sc[:].bitcast(I32), 0)
+            for q in range(QUADS):
+                rows = slice(q * QUAD, (q + 1) * QUAD)
+                spots = eye[rows, q * P : q * P + 2 * (K_PASS + 1)].rearrange("p (t g) -> p t g", t=2)
+                nc.vector.tensor_scalar(
+                    spots[:, :, 0:P:PACK], column[rows, :].rearrange("p (t j) -> p t j", t=2),
+                    row[rows, 0:1], None, EQUAL,
+                )
+            nc.vector.quantize_mx(eye_w[:, 0 : 2 * P].bitcast(FP8X4), eye_sc[:], eye[:, 0 : 2 * K_PASS])
+            halves = eye_w[:].bitcast(U16)
+            nc.vector.tensor_copy(halves[:, 4 * P + 1 :], halves[:, 0 : 4 * P - 1])
 
         def round_cols(raw, grouped, shares):
             for copy, c0, c1 in shares:
@@ -139,7 +144,7 @@ def tile_list_tiert_gelu_kernel(
                 xq[h, a] = (keep([P, HALF], U32, f"xq_w{h}{a}"), keep([P, HALF], U8, f"xq_sc{h}{a}"))
                 xr[h, a] = (keep([P, HALF], U32, f"xr_w{h}{a}"), keep([P, HALF], U8, f"xr_sc{h}{a}"))
             words, scales = xq[h, a]
-            grouped = keep([P, UNIT, PACK], BF16, f"xq_bf{h}{a}{2 * u}")
+            grouped = keep([P, UNIT, PACK], BF16, f"xq_bf{h}{a}{2 * u}", "xq_bf002" if (h, a) == (0, 0) else None)
             round_cols(x_raw[h, a, "unit", u], grouped, shares)
             cols = slice(u * UNIT, (u + 1) * UNIT)
             return lambda: quantize(grouped[:], words[:, cols], scales[:, cols])
@@ -154,7 +159,7 @@ def tile_list_tiert_gelu_kernel(
                 nc.tensor.matmul_mx(
                     back[:, t, :],
                     lhsT=eye_w[:, t * P : (t + 1) * P].bitcast(FP8X4),
-                    lhsT_scale=eye_sc[:, t * P : (t + 1) * P],
+                    lhsT_scale=eye_sc[:, t % 2 * P : (t % 2 + 1) * P],
                     rhs=words[:, cols].bitcast(FP8X4),
                     rhs_scale=scales[:, cols],
                     start=True,
@@ -233,7 +238,7 @@ def tile_list_tiert_gelu_kernel(
                     nc.sync.dma_start(out[n * P : (n + 1) * P, h * HALF : (h + 1) * HALF][:, cols], result[:, cols])
 
         parked = {}
-        spare = [f"xq_bf{h}{a}{s}" for h in (1, 0) for a in (1, 0) for s in (2, 0)]
+        spare = [f"xq_bf{h}{a}{s}" for h in (1, 0) for a in (1, 0) for s in (2, 0)][:-1]
         bank_of = {}
 
         def x_passes(tiles, steps):
@@ -253,17 +258,13 @@ def tile_list_tiert_gelu_kernel(
                     add_pass(
                         h, n, bank_of[h, n],
                         words.bitcast(FP8X4), scales,
-                        tab_w[h][:, a, :].bitcast(FP4X4), tab_sc[a][:, h * HALF : (h + 1) * HALF],
+                        tab_w[h][:, a, :].bitcast(FP4X4), tab_sc[:, a, h * HALF : (h + 1) * HALF],
                     )
 
         every_x = ((xq, 0), (xr, 0), (xq, 1), (xr, 1))
         S, V = on_scalar, on_vector
 
-        nc.vector.memset(b_rows[:], 0.0)
-        nc.vector.memset(wx_sc[:].bitcast(I32), 0)
-        nc.vector.memset(scale_window[0:first_row, :].bitcast(I32), 0)
         make_eye()
-        nc.sync.dma_start(b_rows[0 : N // P, :], b.rearrange("(c p) -> c p", p=P))
         load_x(0, 0, 0, 256)
         load_x(0, 0, 256, 256)
         load_wx(0)
@@ -273,38 +274,42 @@ def tile_list_tiert_gelu_kernel(
         load_wx(1)
         load_x(1, 0, 0, 512)
         load_x(1, 1, 0, 512)
-        nc.sync.dma_start(offsets[:], offs)
-        load_tab_scales()
-        for a in range(PASSES):
-            nc.vector.memset(tab_sc[a][:].bitcast(I32), 0)
-        load_wt(0, 0, 2)
-        load_wt(1, 0, 2)
-        load_table()
-        for n0 in (2, 4):
-            load_wt(0, n0, 2)
-            load_wt(1, n0, 2)
-
+        with nc.allow_non_contiguous_dma(reason="one bias value a partition and tile"):
+            nc.sync.dma_start(bias[:], b.rearrange("(c p) -> p c", p=P))
         def tiles(h, *ns):
             return [(h, n) for n in ns]
         def place(ts, banks):
             for tile, bank in zip(ts, banks):
                 bank_of[tile] = bank
         whole = lambda copy: ((copy, 0, UNIT),)
-        make_bias(5)
         early = tiles(0, 4, 5, 6, 7, 2, 3)
         place(early, (2, 3, 4, 5, 0, 1))
         parked.update({tile: None for tile in early})
         for u in range(2):
-            round_x(0, 0, u, ((S, 0, 96), (V, 96, UNIT)))()
+            finish = round_x(0, 0, u, ((S, 0, 96), (V, 96, UNIT)))
+            finish()
         for s, bank in enumerate((0, 1, 6, 7)):
             take_back(0, 0, s, bank)
             if s > 0:
                 quantize_left(0, 0, s - 1, s)
         quantize_left(0, 0, 3, 4)
+        tab_sc = keep([P, PASSES, J], U8, "tab_sc", "x_raw000")
+        nc.gpsimd.memset(tab_sc[:].bitcast(I32), 0)
         for u in range(2):
             round_x(0, 1, u, whole(S))()
         for s, bank in enumerate((1, 6, 7, 1)):
             take_back(0, 1, s, bank)
+        scale_window = keep([P, T], U8, "scale_window", "x_raw010")
+        nc.gpsimd.memset(scale_window[0:first_row, :].bitcast(I32), 0)
+        load_wt(0, 0, 2)
+        load_wt(1, 0, 2)
+        nc.sync.dma_start(offsets[:], offs)
+        load_tab_scales()
+        load_table()
+        for n0 in (2, 4):
+            load_wt(0, n0, 2)
+            load_wt(1, n0, 2)
+
         third = [round_x(1, 0, u, whole(S)) for u in range(2)]
         third[0]()
         quantize_left(0, 1)
@@ -315,9 +320,9 @@ def tile_list_tiert_gelu_kernel(
         take_back(1, 0, 2, 6)
         take_back(1, 0, 3, 7)
         x_passes(early[:5], every_x[:1])
-        quarter_passes(early[:4], xr, 0)
+        quarter_passes(early[:2], xr, 0)
         x_passes(early[:5], every_x[2:3])
-        x_passes(early[4:5], every_x[1:2])
+        x_passes(early[2:5], every_x[1:2])
         x_passes(early[5:], every_x[:3])
         x_passes(early[:2], every_x[3:])
 
@@ -329,7 +334,7 @@ def tile_list_tiert_gelu_kernel(
             take_back(1, 1, s, bank)
         first_pair = [round_wt(a, 0, 0, 2, whole(S)) for a in range(2)]
 
-        picked_sc = gather_scales("x_raw110")
+        picked_sc = gather_scales("x_raw100")
         move_scales(picked_sc, 1, nc.sync)
         move_scales(picked_sc, 0, nc.sync)
         load_wt(0, 6, 2)

@@ -66,6 +66,8 @@ def tile_list_tiert_gelu_kernel(
         wx_sc = keep([P, PASSES, N], U8, "wx_sc")
         word_window = keep([P, T], U32, "word_window")
         bias = keep([P, N // P], F32, "bias")
+        b_rows = keep([P, P], F32, "b_rows")
+        identity = keep([P, P], F32, "identity")
         eye_w = keep([P, PACK * P], U32, "eye_w")
         eye_sc = keep([P, 2 * P], U8, "eye_sc")
         first_row = P - SCALE_ROWS
@@ -130,8 +132,14 @@ def tile_list_tiert_gelu_kernel(
                     row[rows, 0:1], None, EQUAL,
                 )
             nc.vector.quantize_mx(eye_w[:, 0 : 2 * P].bitcast(FP8X4), eye_sc[:], eye[:, 0 : 2 * K_PASS])
+            nc.scalar.copy(identity[:], eye[:, 0:K_PASS:PACK])
             halves = eye_w[:].bitcast(U16)
             nc.vector.tensor_copy(halves[:, 4 * P + 1 :], halves[:, 0 : 4 * P - 1])
+
+        def make_bias(bank):
+            b_bank = psum.tile([P, PACK, P], F32, name="b_bank", tag=f"bank{bank}")
+            nc.tensor.transpose(b_bank[:, 0, :], b_rows[:], identity[:])
+            nc.scalar.copy(bias[:], b_bank[:, 0, 0 : N // P])
 
         def round_cols(raw, grouped, shares):
             for copy, c0, c1 in shares:
@@ -230,15 +238,27 @@ def tile_list_tiert_gelu_kernel(
                 if split:
                     total = parked[h, n]
                     nc.vector.tensor_tensor(total[:], total[:], acc[h, n][:], ADD)
-                result = keep([P, HALF], F32, f"result{h}{n}", spare.pop() if spare else None)
-                parts = 2 if (h, n) == (1, N // P - 1) else 1
-                for part in range(parts):
-                    cols = slice(part * HALF // parts, (part + 1) * HALF // parts)
-                    nc.scalar.activation(result[:, cols], total[:, cols], GELU, bias=bias[:, n : n + 1])
-                    nc.sync.dma_start(out[n * P : (n + 1) * P, h * HALF : (h + 1) * HALF][:, cols], result[:, cols])
+                if (h, n) in alone:
+                    result = keep([P, HALF], F32, f"result{h}{n}", spare.pop() if spare else None)
+                    parts = 2 if (h, n) == (1, N // P - 1) else 1
+                    for part in range(parts):
+                        cols = slice(part * HALF // parts, (part + 1) * HALF // parts)
+                        nc.scalar.activation(result[:, cols], total[:, cols], GELU, bias=bias[:, n : n + 1])
+                        nc.sync.dma_start(
+                            out[n * P : (n + 1) * P, h * HALF : (h + 1) * HALF][:, cols], result[:, cols]
+                        )
+                else:
+                    if n % 2 == 0:
+                        results[h, n // 2] = keep([P, 2, HALF], F32, f"result{h}{n}", spare.pop())
+                    result = results[h, n // 2]
+                    nc.scalar.activation(result[:, n % 2, :], total[:], GELU, bias=bias[:, n : n + 1])
+                    if n % 2 == 1:
+                        rows = out[(n - 1) * P : (n + 1) * P, h * HALF : (h + 1) * HALF]
+                        nc.sync.dma_start(rows.rearrange("(i p) j -> p i j", p=P), result[:])
 
         parked = {}
-        spare = [f"xq_bf{h}{a}{s}" for h in (1, 0) for a in (1, 0) for s in (2, 0)][:-1]
+        spare = ["x_raw012", "x_raw002", "x_raw110", "xq_bf112", "xq_bf102", "xq_bf012", "xq_bf002"]
+        results, alone = {}, [(h, n) for h in range(2) for n in range(8)]
         bank_of = {}
 
         def x_passes(tiles, steps):
@@ -264,8 +284,10 @@ def tile_list_tiert_gelu_kernel(
         every_x = ((xq, 0), (xr, 0), (xq, 1), (xr, 1))
         S, V = on_scalar, on_vector
 
+        nc.vector.memset(b_rows[:], 0.0)
         make_eye()
         load_x(0, 0, 0, 256)
+        nc.sync.dma_start(b_rows[0 : N // P, :], b.rearrange("(c p) -> c p", p=P))
         load_x(0, 0, 256, 256)
         load_wx(0)
         load_wx_scales(nc.sync)
@@ -274,14 +296,13 @@ def tile_list_tiert_gelu_kernel(
         load_wx(1)
         load_x(1, 0, 0, 512)
         load_x(1, 1, 0, 512)
-        with nc.allow_non_contiguous_dma(reason="one bias value a partition and tile"):
-            nc.sync.dma_start(bias[:], b.rearrange("(c p) -> p c", p=P))
         def tiles(h, *ns):
             return [(h, n) for n in ns]
         def place(ts, banks):
             for tile, bank in zip(ts, banks):
                 bank_of[tile] = bank
         whole = lambda copy: ((copy, 0, UNIT),)
+        make_bias(5)
         early = tiles(0, 4, 5, 6, 7, 2, 3)
         place(early, (2, 3, 4, 5, 0, 1))
         parked.update({tile: None for tile in early})
@@ -301,14 +322,11 @@ def tile_list_tiert_gelu_kernel(
             take_back(0, 1, s, bank)
         scale_window = keep([P, T], U8, "scale_window", "x_raw010")
         nc.gpsimd.memset(scale_window[0:first_row, :].bitcast(I32), 0)
-        load_wt(0, 0, 2)
-        load_wt(1, 0, 2)
         nc.sync.dma_start(offsets[:], offs)
         load_tab_scales()
+        load_wt(0, 0, 4)
+        load_wt(1, 0, 4)
         load_table()
-        for n0 in (2, 4):
-            load_wt(0, n0, 2)
-            load_wt(1, n0, 2)
 
         third = [round_x(1, 0, u, whole(S)) for u in range(2)]
         third[0]()
@@ -328,17 +346,17 @@ def tile_list_tiert_gelu_kernel(
 
         x_passes(early[2:], every_x[3:])
         fourth[0]()
-        quantize_left(1, 0)
         fourth[1]()
+        quantize_left(1, 0)
         for s, bank in enumerate((4, 5, 6, 7)):
             take_back(1, 1, s, bank)
         first_pair = [round_wt(a, 0, 0, 2, whole(S)) for a in range(2)]
 
         picked_sc = gather_scales("x_raw100")
         move_scales(picked_sc, 1, nc.sync)
+        load_wt(0, 4, 4)
         move_scales(picked_sc, 0, nc.sync)
-        load_wt(0, 6, 2)
-        load_wt(1, 6, 2)
+        load_wt(1, 4, 4)
         quantize_left(1, 1)
         first_pair[0]()
         part = gather_words(1)
@@ -348,17 +366,16 @@ def tile_list_tiert_gelu_kernel(
         x_passes(tiles(0, 0, 1), every_x)
         place(tiles(1, 0, 1, 2, 3, 4, 5), (0, 1, 4, 5, 6, 7))
         x_passes(tiles(1, 0, 1, 2, 3, 4, 5), every_x)
-        second_pair = [round_wt(a, 2, 0, 2, whole(S)) for a in range(2)]
+        second_pair = [round_wt(a, 0, 2, 2, whole(S)) for a in range(2)]
         second_pair[0]()
         part = gather_words(0)
         second_pair[1]()
         part()
-        third_pair = [round_wt(a, 4, 0, 2, whole(S)) for a in range(2)]
-        for finish in third_pair:
-            finish()
+        for off in (0, 2):
+            round_wt(0, 4, off, 2, whole(S))()
         tab_passes(tiles(1, 0, 1))
         tab_passes(tiles(1, 2, 3))
-        last_pair = [round_wt(a, 6, 0, 2, whole(V)) for a in range(2)]
+        last_pair = [round_wt(a, 4, off, 2, whole(V)) for a, off in ((1, 0), (1, 2))]
         for finish in last_pair:
             finish()
         tab_passes(tiles(0, 0, 1))

@@ -209,7 +209,7 @@ def tile_list_tiert_gelu_kernel(
             return picked_sc
 
         def gather_words(h):
-            picked = keep([P, HALF], U32, f"picked_w{h}", "picked_w")
+            picked = keep([P, HALF], U32, f"picked_w{h}")
             entries = offsets[:, h * HALF // LIST_ROWS : (h + 1) * HALF // LIST_ROWS]
             nc.vector.tensor_copy(picked[:], word_window[:].indirect(entries))
             tab_w[h] = keep([P, PASSES, 2 * HALF], U8, f"tab_w{h}")
@@ -257,7 +257,7 @@ def tile_list_tiert_gelu_kernel(
                         nc.sync.dma_start(rows.rearrange("(i p) j -> p i j", p=P), result[:])
 
         parked = {}
-        spare = ["x_raw012", "x_raw002", "x_raw110", "xq_bf112", "xq_bf102", "xq_bf012", "xq_bf002"]
+        spare = ["x_raw012", "x_raw002", "x_raw100", "xq_bf112", "xq_bf102", "xq_bf012", "xq_bf002"]
         results, alone = {}, [(h, n) for h in range(2) for n in range(8)]
         bank_of = {}
 
@@ -295,7 +295,8 @@ def tile_list_tiert_gelu_kernel(
         load_x(0, 1, 256, 256)
         load_wx(1)
         load_x(1, 0, 0, 512)
-        load_x(1, 1, 0, 512)
+        load_x(1, 1, 0, 256)
+        load_x(1, 1, 256, 256)
         def tiles(h, *ns):
             return [(h, n) for n in ns]
         def place(ts, banks):
@@ -325,8 +326,10 @@ def tile_list_tiert_gelu_kernel(
         nc.sync.dma_start(offsets[:], offs)
         load_tab_scales()
         load_wt(0, 0, 4)
-        load_wt(1, 0, 4)
+        load_wt(1, 0, 2)
         load_table()
+        load_wt(1, 2, 2)
+        load_wt(0, 4, 4)
 
         third = [round_x(1, 0, u, whole(S)) for u in range(2)]
         third[0]()
@@ -348,17 +351,18 @@ def tile_list_tiert_gelu_kernel(
         fourth[0]()
         fourth[1]()
         quantize_left(1, 0)
-        for s, bank in enumerate((4, 5, 6, 7)):
-            take_back(1, 1, s, bank)
+        take_back(1, 1, 0, 4)
+        take_back(1, 1, 1, 5)
+        picked_sc = gather_scales("x_raw110")
+        take_back(1, 1, 2, 6)
+        take_back(1, 1, 3, 7)
         first_pair = [round_wt(a, 0, 0, 2, whole(S)) for a in range(2)]
 
-        picked_sc = gather_scales("x_raw100")
         move_scales(picked_sc, 1, nc.sync)
-        load_wt(0, 4, 4)
         move_scales(picked_sc, 0, nc.sync)
         load_wt(1, 4, 4)
-        quantize_left(1, 1)
         first_pair[0]()
+        quantize_left(1, 1)
         part = gather_words(1)
         first_pair[1]()
         part()
@@ -366,17 +370,17 @@ def tile_list_tiert_gelu_kernel(
         x_passes(tiles(0, 0, 1), every_x)
         place(tiles(1, 0, 1, 2, 3, 4, 5), (0, 1, 4, 5, 6, 7))
         x_passes(tiles(1, 0, 1, 2, 3, 4, 5), every_x)
-        second_pair = [round_wt(a, 0, 2, 2, whole(S)) for a in range(2)]
+        second_pair = [round_wt(0, 0, 2, 2, whole(S)), round_wt(1, 2, 0, 2, whole(S))]
         second_pair[0]()
         part = gather_words(0)
         second_pair[1]()
         part()
-        for off in (0, 2):
-            round_wt(0, 4, off, 2, whole(S))()
+        late_0 = [round_wt(0, 4, off, 2, whole(S)) for off in (0, 2)]
         tab_passes(tiles(1, 0, 1))
         tab_passes(tiles(1, 2, 3))
-        last_pair = [round_wt(a, 4, off, 2, whole(V)) for a, off in ((1, 0), (1, 2))]
-        for finish in last_pair:
+        for i, off in enumerate((0, 2)):
+            finish = round_wt(1, 4, off, 2, whole(V))
+            late_0[i]()
             finish()
         tab_passes(tiles(0, 0, 1))
         place(tiles(0, 2, 3), (0, 1))

@@ -150,7 +150,6 @@ def tile_list_tiert_gelu_kernel(
         def round_x(h, a, u, shares):
             if (h, a) not in xq:
                 xq[h, a] = (keep([P, HALF], U32, f"xq_w{h}{a}"), keep([P, HALF], U8, f"xq_sc{h}{a}"))
-                xr[h, a] = (keep([P, HALF], U32, f"xr_w{h}{a}"), keep([P, HALF], U8, f"xr_sc{h}{a}"))
             words, scales = xq[h, a]
             grouped = keep([P, UNIT, PACK], BF16, f"xq_bf{h}{a}{2 * u}", "xq_bf002" if (h, a) == (0, 0) else None)
             round_cols(x_raw[h, a, "unit", u], grouped, shares)
@@ -176,6 +175,9 @@ def tile_list_tiert_gelu_kernel(
             nc.vector.tensor_tensor(interleaved(left[h, a][:, cols, :]), planar(x_raw[h, a, s]), planar(back[:]), SUB)
 
         def quantize_left(h, a, first=0, end=HALF // P):
+            if first == 0:
+                behind = "xq_bf100" if (h, a) == (0, 1) else None
+                xr[h, a] = (keep([P, HALF], U32, f"xr_w{h}{a}", behind), keep([P, HALF], U8, f"xr_sc{h}{a}"))
             words, scales = xr[h, a]
             cols = slice(first * P, end * P)
             quantize(left[h, a][:, cols, :], words[:, cols], scales[:, cols])
@@ -329,7 +331,7 @@ def tile_list_tiert_gelu_kernel(
         load_wt(1, 0, 2)
         load_table()
         load_wt(1, 2, 2)
-        load_wt(0, 4, 4)
+        load_wt(0, 4, 2)
 
         third = [round_x(1, 0, u, whole(S)) for u in range(2)]
         third[0]()
@@ -359,6 +361,7 @@ def tile_list_tiert_gelu_kernel(
         first_pair = [round_wt(a, 0, 0, 2, whole(S)) for a in range(2)]
 
         move_scales(picked_sc, 1, nc.sync)
+        load_wt(0, 6, 2)
         move_scales(picked_sc, 0, nc.sync)
         load_wt(1, 4, 4)
         first_pair[0]()
@@ -375,7 +378,7 @@ def tile_list_tiert_gelu_kernel(
         part = gather_words(0)
         second_pair[1]()
         part()
-        late_0 = [round_wt(0, 4, off, 2, whole(S)) for off in (0, 2)]
+        late_0 = [round_wt(0, n0, 0, 2, whole(S)) for n0 in (4, 6)]
         tab_passes(tiles(1, 0, 1))
         tab_passes(tiles(1, 2, 3))
         for i, off in enumerate((0, 2)):

@@ -119,6 +119,8 @@ def tile_list_tiert_gelu_kernel(
             nc.vector.memset(flags[:, 0 : two + QUAD], 1.0)
             nc.vector.memset(flags[:, two + QUAD : two + QUAD + 1], 0.0)
             nc.vector.memset(flags[:, two + QUAD + 1 :], 1.0)
+            unread = keep([P, 1], F32, "unread")
+            nc.scalar.activation(unread[:], flags[:, 0:1], GELU)
             nc.vector.memset(eye[:, 0 : 2 * K_PASS].bitcast(I32), 0)
             nc.vector.tensor_tensor_scan(column[:], flags[:, two:], flags[:, 0:two], 0.0, MULT, ADD)
             nc.vector.memset(eye_w[:, 2 * P :], 0)

from contextlib import ExitStack

import concourse.mybir as mybir

K, L, N, T, J = 1024, 1024, 1024, 4096, 1024
FLOPS = 2 * N * J * (K + 2 * L) + 2 * 512 * L * J

F32 = mybir.dt.float32
BF16 = mybir.dt.bfloat16
I32 = mybir.dt.int32
U32 = mybir.dt.uint32
U16 = mybir.dt.uint16
U8 = mybir.dt.uint8
FP8X4 = mybir.dt.float8_e4m3fn_x4
FP4X4 = mybir.dt.float4_e2m1fn_x4
GELU = mybir.ActivationFunctionType.Gelu_apprx_tanh
SUB = mybir.AluOpType.subtract
ADD = mybir.AluOpType.add
MULT = mybir.AluOpType.mult
EQUAL = mybir.AluOpType.is_equal

P = 128
PACK = 4
K_PASS = P * PACK
PASSES = 2
QUADS = 4
QUAD = 32
HALF = 512
UNIT = 256
LIST_ROWS = 16
SCALE_ROWS = PASSES * K_PASS // 32
ALIGN = 256


def interleaved(ap):
    return ap.rearrange("p (c i) t -> p c t i", i=4)


def planar(ap):
    return ap.rearrange("p t (c i) -> p c t i", i=4)


def tile_list_tiert_gelu_kernel(
    tc, tab_words, tab_scales, wt, x, wx_words, wx_scales, b, offs, out
):
    nc = tc.nc
    with ExitStack() as ctx:
        held = ctx.enter_context(tc.tile_pool(name="held", bufs=1))
        psum = ctx.enter_context(tc.psum_pool(name="psum", bufs=1))
        on_scalar, on_vector = nc.scalar.copy, nc.vector.tensor_copy

        def keep(shape, dtype, name, reuse=None):
            return held.tile(shape, dtype, name=name, tag=reuse or name, align_bytes=ALIGN)

        def load_rows(src, a, col0, width, name):
            raw = keep([P, PACK, width], F32, name)
            rows = src[a * K_PASS : (a + 1) * K_PASS, col0 : col0 + width]
            nc.sync.dma_start(raw[:], rows.rearrange("(p t) w -> p t w", t=PACK))
            return raw

        def quantize(grouped, words, scales):
            nc.vector.quantize_mx(words.bitcast(FP8X4), scales, grouped.rearrange("p w t -> p (w t)"))

        offsets = held.tile([P, J // LIST_ROWS], U16, name="offsets")
        wx_w = [keep([P, 2 * N], U8, f"wx_w{a}") for a in range(PASSES)]
        wx_sc = keep([P, PASSES, N], U8, "wx_sc")
        word_window = keep([P, T], U32, "word_window")
        bias = keep([P, N // P], F32, "bias")
        b_rows = keep([P, P], F32, "b_rows")
        identity = keep([P, P], F32, "identity")
        eye_w = keep([P, PACK * P], U32, "eye_w")
        eye_sc = keep([P, 2 * P], U8, "eye_sc")
        first_row = P - SCALE_ROWS
        x_raw, wt_raw = {}, {}
        xq, xr, wq, tab_w = {}, {}, {}, {}
        acc, done = {}, {}

        def load_x(h, a, col0, width):
            raw = load_rows(x, a, h * HALF + col0, width, f"x_raw{h}{a}{col0 // P}")
            for s in range(width // P):
                x_raw[h, a, col0 // P + s] = raw[:, :, s * P : (s + 1) * P]
            for u in range(width // UNIT):
                x_raw[h, a, "unit", col0 // UNIT + u] = raw[:, :, u * UNIT : (u + 1) * UNIT]

        def load_wt(a, n0, tiles):
            wt_raw[a, n0] = load_rows(wt, a, n0 * P, tiles * P, f"wt_raw{a}{n0}")

        def load_wx(a):
            nc.sync.dma_start(wx_w[a][:].bitcast(I32), wx_words[a].bitcast(I32))

        def load_wx_scales(queue):
            for r in range(4):
                queue.dma_start(
                    wx_sc[r:P:32, :, :].bitcast(I32),
                    wx_scales[:, r:16:4, :].rearrange("a q n -> q a n").bitcast(I32),
                )

        def load_tab_scales():
            nc.sync.dma_start(
                scale_window[first_row:P, :].bitcast(I32), tab_scales.rearrange("a q t -> (a q) t").bitcast(I32)
            )

        def load_table():
            nc.sync.dma_start(word_window[:].bitcast(I32), tab_words[0].rearrange("p t c -> p (t c)").bitcast(I32))

        def move_scales(picked_sc, a, queue):
            for r in range(4):
                row = first_row + 16 * a + r
                queue.dma_start(
                    tab_sc[r:P:32, a, :].bitcast(I32), picked_sc[row : row + 13 : 4, :].bitcast(I32)
                )

        def make_eye():
            two = 2 * QUAD
            flags = keep([P, 2 * two], F32, "flags")
            column = keep([P, two], F32, "column")
            row = keep([P, QUAD], F32, "row")
            eye = keep([P, 3 * K_PASS], BF16, "eye")
            nc.vector.memset(flags[:, 0 : two + QUAD], 1.0)
            nc.vector.memset(flags[:, two + QUAD : two + QUAD + 1], 0.0)
            nc.vector.memset(flags[:, two + QUAD + 1 :], 1.0)
            unread = keep([P, 1], F32, "unread")
            nc.scalar.activation(unread[:], flags[:, 0:1], GELU)
            nc.vector.memset(eye[:, 0 : 2 * K_PASS].bitcast(I32), 0)
            nc.vector.tensor_tensor_scan(column[:], flags[:, two:], flags[:, 0:two], 0.0, MULT, ADD)
            nc.vector.memset(eye_w[:, 2 * P :], 0)
            nc.vector.transpose(row[:], column[:, 0:QUAD])
            nc.vector.memset(wx_sc[:].bitcast(I32), 0)
            for q in range(QUADS):
                rows = slice(q * QUAD, (q + 1) * QUAD)
                spots = eye[rows, q * P : q * P + 2 * (K_PASS + 1)].rearrange("p (t g) -> p t g", t=2)
                nc.vector.tensor_scalar(
                    spots[:, :, 0:P:PACK], column[rows, :].rearrange("p (t j) -> p t j", t=2),
                    row[rows, 0:1], None, EQUAL,
                )
            nc.vector.quantize_mx(eye_w[:, 0 : 2 * P].bitcast(FP8X4), eye_sc[:], eye[:, 0 : 2 * K_PASS])
            nc.scalar.copy(identity[:], eye[:, 0:K_PASS:PACK])
            halves = eye_w[:].bitcast(U16)
            nc.vector.tensor_copy(halves[:, 4 * P + 1 :], halves[:, 0 : 4 * P - 1])

        def make_bias(bank):
            b_bank = psum.tile([P, PACK, P], F32, name="b_bank", tag=f"bank{bank}")
            nc.tensor.transpose(b_bank[:, 0, :], b_rows[:], identity[:])
            nc.scalar.copy(bias[:], b_bank[:, 0, 0 : N // P])

        def round_cols(raw, grouped, shares):
            for copy, c0, c1 in shares:
                copy(interleaved(grouped[:, c0:c1, :]), planar(raw[:, :, c0:c1]))

        left = {}

        def round_x(h, a, u, shares):
            if (h, a) not in xq:
                xq[h, a] = (keep([P, HALF], U32, f"xq_w{h}{a}"), keep([P, HALF], U8, f"xq_sc{h}{a}"))
            words, scales = xq[h, a]
            grouped = keep([P, UNIT, PACK], BF16, f"xq_bf{h}{a}{2 * u}", "xq_bf002" if (h, a) == (0, 0) else None)
            round_cols(x_raw[h, a, "unit", u], grouped, shares)
            cols = slice(u * UNIT, (u + 1) * UNIT)
            return lambda: quantize(grouped[:], words[:, cols], scales[:, cols])

        def take_back(h, a, s, bank):
            words, scales = xq[h, a]
            if s == 0:
                left[h, a] = keep([P, HALF, PACK], BF16, f"left{h}{a}", f"xq_bf{h}{a}2")
            cols = slice(s * P, (s + 1) * P)
            back = psum.tile([P, PACK, P], F32, name="back", tag=f"bank{bank}")
            for t in range(PACK):
                nc.tensor.matmul_mx(
                    back[:, t, :],
                    lhsT=eye_w[:, t * P : (t + 1) * P].bitcast(FP8X4),
                    lhsT_scale=eye_sc[:, t % 2 * P : (t % 2 + 1) * P],
                    rhs=words[:, cols].bitcast(FP8X4),
                    rhs_scale=scales[:, cols],
                    start=True,
                    stop=True,
                )
            nc.vector.tensor_tensor(interleaved(left[h, a][:, cols, :]), planar(x_raw[h, a, s]), planar(back[:]), SUB)

        def quantize_left(h, a, first=0, end=HALF // P):
            if first == 0:
                behind = "xq_bf100" if (h, a) == (0, 1) else None
                xr[h, a] = (keep([P, HALF], U32, f"xr_w{h}{a}", behind), keep([P, HALF], U8, f"xr_sc{h}{a}"))
            words, scales = xr[h, a]
            cols = slice(first * P, end * P)
            quantize(left[h, a][:, cols, :], words[:, cols], scales[:, cols])

        def quarter_passes(tiles, tier, a):
            for s in range(HALF // P):
                cols = slice(s * P, (s + 1) * P)
                for h, n in tiles:
                    words, scales = tier[h, a]
                    nc.tensor.matmul_mx(
                        acc[h, n][:, cols],
                        lhsT=wx_w[a][:, 2 * n * P : 2 * (n + 1) * P].bitcast(FP4X4),
                        lhsT_scale=wx_sc[:, a, n * P : (n + 1) * P],
                        rhs=words[:, cols].bitcast(FP8X4), rhs_scale=scales[:, cols], start=False, stop=False,
                    )
            for tile in tiles:
                done[tile] = done[tile] + 1

        def round_wt(a, n0, off, tiles, shares, reuse=None):
            name = f"wq{a}{n0 + off}"
            words, scales = keep([P, tiles * P], U32, name + "_w"), keep([P, tiles * P], U8, name + "_sc")
            grouped = keep([P, tiles * P, PACK], BF16, name + "_bf", reuse)
            round_cols(wt_raw[a, n0][:, :, off * P : (off + tiles) * P], grouped, shares)
            for i in range(tiles):
                wq[n0 + off + i, a] = (words[:, i * P : (i + 1) * P], scales[:, i * P : (i + 1) * P])
            return lambda: quantize(grouped[:], words[:], scales[:])

        def gather_scales(reuse):
            picked_sc = keep([P, J], U8, "picked_sc", reuse)
            nc.vector.tensor_copy(picked_sc[:], scale_window[:].indirect(offsets[:]))
            return picked_sc

        def gather_words(h):
            picked = keep([P, HALF], U32, f"picked_w{h}")
            entries = offsets[:, h * HALF // LIST_ROWS : (h + 1) * HALF // LIST_ROWS]
            nc.vector.tensor_copy(picked[:], word_window[:].indirect(entries))
            tab_w[h] = keep([P, PASSES, 2 * HALF], U8, f"tab_w{h}")
            return lambda: nc.vector.tensor_copy(
                tab_w[h][:].bitcast(U16), picked[:].bitcast(U16).rearrange("p (j a) -> p a j", a=PASSES)
            )

        def add_pass(h, n, bank, lhsT, lhsT_scale, rhs, rhs_scale):
            count = done.get((h, n), 0)
            split = (h, n) in parked
            first = count == 0 or (split and count == 2 * PASSES)
            last = count == 3 * PASSES - 1
            park = split and count == 2 * PASSES - 1
            if first:
                acc[h, n] = psum.tile([P, HALF], F32, name=f"acc{h}{n}", tag=f"bank{bank}")
            nc.tensor.matmul_mx(
                acc[h, n][:], lhsT=lhsT, lhsT_scale=lhsT_scale, rhs=rhs, rhs_scale=rhs_scale,
                start=first, stop=last or park,
            )
            done[h, n] = count + 1
            if park:
                parked[h, n] = keep([P, HALF], F32, f"parked{h}{n}")
                nc.scalar.copy(parked[h, n][:], acc[h, n][:])
            if last:
                total = acc[h, n]
                if split:
                    total = parked[h, n]
                    nc.vector.tensor_tensor(total[:], total[:], acc[h, n][:], ADD)
                if (h, n) in alone:
                    result = keep([P, HALF], F32, f"result{h}{n}", spare.pop() if spare else None)
                    parts = 2 if (h, n) == (1, N // P - 1) else 1
                    for part in range(parts):
                        cols = slice(part * HALF // parts, (part + 1) * HALF // parts)
                        nc.scalar.activation(result[:, cols], total[:, cols], GELU, bias=bias[:, n : n + 1])
                        nc.sync.dma_start(
                            out[n * P : (n + 1) * P, h * HALF : (h + 1) * HALF][:, cols], result[:, cols]
                        )
                else:
                    if n % 2 == 0:
                        results[h, n // 2] = keep([P, 2, HALF], F32, f"result{h}{n}", spare.pop())
                    result = results[h, n // 2]
                    nc.scalar.activation(result[:, n % 2, :], total[:], GELU, bias=bias[:, n : n + 1])
                    if n % 2 == 1:
                        rows = out[(n - 1) * P : (n + 1) * P, h * HALF : (h + 1) * HALF]
                        nc.sync.dma_start(rows.rearrange("(i p) j -> p i j", p=P), result[:])

        parked = {}
        spare = ["x_raw012", "x_raw002", "x_raw100", "xq_bf112", "xq_bf102", "xq_bf012", "xq_bf002"]
        results, alone = {}, [(h, n) for h in range(2) for n in range(8)]
        bank_of = {}

        def x_passes(tiles, steps):
            for tier, a in steps:
                for h, n in tiles:
                    words, scales = tier[h, a]
                    add_pass(
                        h, n, bank_of[h, n],
                        wx_w[a][:, 2 * n * P : 2 * (n + 1) * P].bitcast(FP4X4), wx_sc[:, a, n * P : (n + 1) * P],
                        words[:].bitcast(FP8X4), scales[:],
                    )

        def tab_passes(tiles, passes=(0, 1)):
            for a in passes:
                for h, n in tiles:
                    words, scales = wq[n, a]
                    add_pass(
                        h, n, bank_of[h, n],
                        words.bitcast(FP8X4), scales,
                        tab_w[h][:, a, :].bitcast(FP4X4), tab_sc[:, a, h * HALF : (h + 1) * HALF],
                    )

        every_x = ((xq, 0), (xr, 0), (xq, 1), (xr, 1))
        S, V = on_scalar, on_vector

        nc.vector.memset(b_rows[:], 0.0)
        make_eye()
        load_x(0, 0, 0, 256)
        nc.sync.dma_start(b_rows[0 : N // P, :], b.rearrange("(c p) -> c p", p=P))
        load_x(0, 0, 256, 256)
        load_wx(0)
        load_wx_scales(nc.sync)
        load_x(0, 1, 0, 256)
        load_x(0, 1, 256, 256)
        load_wx(1)
        load_x(1, 0, 0, 512)
        load_x(1, 1, 0, 256)
        load_x(1, 1, 256, 256)
        def tiles(h, *ns):
            return [(h, n) for n in ns]
        def place(ts, banks):
            for tile, bank in zip(ts, banks):
                bank_of[tile] = bank
        whole = lambda copy: ((copy, 0, UNIT),)
        make_bias(5)
        early = tiles(0, 4, 5, 6, 7, 2, 3)
        place(early, (2, 3, 4, 5, 0, 1))
        parked.update({tile: None for tile in early})
        for u in range(2):
            finish = round_x(0, 0, u, ((S, 0, 96), (V, 96, UNIT)))
            finish()
        for s, bank in enumerate((0, 1, 6, 7)):
            take_back(0, 0, s, bank)
            if s > 0:
                quantize_left(0, 0, s - 1, s)
        quantize_left(0, 0, 3, 4)
        tab_sc = keep([P, PASSES, J], U8, "tab_sc", "x_raw000")
        nc.gpsimd.memset(tab_sc[:].bitcast(I32), 0)
        for u in range(2):
            round_x(0, 1, u, whole(S))()
        for s, bank in enumerate((1, 6, 7, 1)):
            take_back(0, 1, s, bank)
        scale_window = keep([P, T], U8, "scale_window", "x_raw010")
        nc.gpsimd.memset(scale_window[0:first_row, :].bitcast(I32), 0)
        nc.sync.dma_start(offsets[:], offs)
        load_tab_scales()
        load_wt(0, 0, 4)
        load_wt(1, 0, 2)
        load_table()
        load_wt(1, 2, 2)
        load_wt(0, 4, 2)

        third = [round_x(1, 0, u, whole(S)) for u in range(2)]
        third[0]()
        quantize_left(0, 1)
        third[1]()
        take_back(1, 0, 0, 6)
        take_back(1, 0, 1, 7)
        fourth = [round_x(1, 1, u, whole(S)) for u in range(2)]
        take_back(1, 0, 2, 6)
        take_back(1, 0, 3, 7)
        x_passes(early[:5], every_x[:1])
        quarter_passes(early[:2], xr, 0)
        x_passes(early[:5], every_x[2:3])
        x_passes(early[2:5], every_x[1:2])
        x_passes(early[5:], every_x[:3])
        x_passes(early[:2], every_x[3:])

        x_passes(early[2:], every_x[3:])
        fourth[0]()
        fourth[1]()
        quantize_left(1, 0)
        take_back(1, 1, 0, 4)
        take_back(1, 1, 1, 5)
        picked_sc = gather_scales("x_raw110")
        take_back(1, 1, 2, 6)
        take_back(1, 1, 3, 7)
        first_pair = [round_wt(a, 0, 0, 2, whole(S)) for a in range(2)]

        move_scales(picked_sc, 1, nc.sync)
        load_wt(0, 6, 2)
        move_scales(picked_sc, 0, nc.sync)
        load_wt(1, 4, 4)
        first_pair[0]()
        quantize_left(1, 1)
        part = gather_words(1)
        first_pair[1]()
        part()
        place(tiles(0, 0, 1), (2, 3))
        x_passes(tiles(0, 0, 1), every_x)
        place(tiles(1, 0, 1, 2, 3, 4, 5), (0, 1, 4, 5, 6, 7))
        x_passes(tiles(1, 0, 1, 2, 3, 4, 5), every_x)
        second_pair = [round_wt(0, 0, 2, 2, whole(S)), round_wt(1, 2, 0, 2, whole(S))]
        second_pair[0]()
        part = gather_words(0)
        second_pair[1]()
        part()
        late_0 = [round_wt(0, n0, 0, 2, whole(S)) for n0 in (4, 6)]
        tab_passes(tiles(1, 0, 1))
        tab_passes(tiles(1, 2, 3))
        for i, off in enumerate((0, 2)):
            finish = round_wt(1, 4, off, 2, whole(V))
            late_0[i]()
            finish()
        tab_passes(tiles(0, 0, 1))
        place(tiles(0, 2, 3), (0, 1))
        tab_passes(tiles(0, 2, 3))
        tab_passes(tiles(1, 4, 5))
        place(tiles(0, 4, 5, 6, 7) + tiles(1, 6, 7), (4, 5, 2, 3, 0, 1))
        tab_passes(tiles(0, 4, 5))
        tab_passes(tiles(0, 6, 7))
        for n in (6, 7):
            x_passes(tiles(1, n), every_x)
            tab_passes(tiles(1, n))
